import numpy as np
import ml_dtypes


def mxq(x, axis, fmt="e4m3"):
    dtype, down = {"e4m3": (ml_dtypes.float8_e4m3fn, 7), "e5m2": (ml_dtypes.float8_e5m2, 14)}[fmt]
    v = np.moveaxis(np.asarray(x, np.float32).astype(ml_dtypes.bfloat16).astype(np.float64), axis, -1)
    blocks = v.reshape(v.shape[:-1] + (-1, 32))
    amax = np.abs(blocks).max(-1, keepdims=True)
    byte = np.maximum(np.where(amax > 0, np.frexp(amax)[1] - 1 + 127, 0) - down, 1)
    scale = np.exp2(byte - 127.0)
    codes = (blocks / scale).astype(np.float32).astype(dtype).astype(np.float64)
    return np.moveaxis((codes * scale).reshape(v.shape), -1, axis)


WIDE = False


def mx_kscale(k):
    if not WIDE:
        return np.ones(k)
    levels = np.array([10, -10, 5, -5, 0])
    if k % 512:
        return np.exp2(np.random.permutation(np.resize(levels, k // 32))).repeat(32)
    a = np.empty((k // 512, 16))
    for p in range(k // 512):
        a[p, :8] = np.random.permutation(np.resize(levels, 8))
        for g in range(8):
            far = levels[np.abs(levels - a[p, g]) >= 10]
            a[p, g + 8] = far[np.random.randint(len(far))]
    return np.exp2(a.ravel()).repeat(32)


BF16 = ml_dtypes.bfloat16


def bf(x):
    return np.asarray(x, np.float32).astype(BF16)


def f64(x):
    return np.asarray(x).astype(np.float64)


E2M1 = np.array([0.0, 0.5, 1.0, 1.5, 2.0, 3.0, 4.0, 6.0, -0.0, -0.5, -1.0, -1.5, -2.0, -3.0, -4.0, -6.0])


def pack_weight(w, fmt):
    k, n = w.shape
    w = f64(bf(w)).reshape(k // 32, 32, n)
    amax = np.abs(w).max(1)
    if fmt == "e4m3":
        byte = np.frexp(amax)[1] - 1 + 127 - 7
    else:
        mant, ex = np.frexp(amax / 6.0)
        byte = np.where(mant > 0.5, ex, ex - 1) + 127
    byte = np.clip(np.where(amax > 0, byte, 1), 1, 254)
    scaled = (w * np.exp2(127.0 - byte)[:, None, :]).reshape(k, n).astype(np.float32)
    by_word = np.ascontiguousarray(scaled.reshape(k // 512, 128, 4, n).transpose(0, 1, 3, 2))
    if fmt == "e4m3":
        words = by_word.astype(ml_dtypes.float8_e4m3fn).view(np.uint8)
    else:
        c = by_word.astype(ml_dtypes.float4_e2m1fn).view(np.uint8) & 0xF
        words = c[..., 0::2] | (c[..., 1::2] << 4)
    return np.ascontiguousarray(words), np.ascontiguousarray(byte.astype(np.uint8).reshape(k // 512, 16, n))


def unpack_weight(words, scales, fmt):
    g, p, n, _ = words.shape
    if fmt == "e4m3":
        vals = np.ascontiguousarray(words).view(ml_dtypes.float8_e4m3fn).astype(np.float64)
    else:
        nib = np.empty((g, p, n, 4), np.uint8)
        nib[..., 0::2] = words & 0xF
        nib[..., 1::2] = words >> 4
        vals = E2M1[nib]
    vals = vals * np.repeat(np.exp2(scales.astype(np.float64) - 127.0), 8, axis=1)[..., None]
    return vals.transpose(0, 1, 3, 2).reshape(g * 512, n)
def pack4(w):
    words, scales = pack_weight(w, "e2m1")
    return words.reshape(words.shape[0], 128, -1), scales


def unpack4(words, scales):
    return unpack_weight(words.reshape(words.shape[0], 128, -1, 2), scales, "e2m1")


F, R1, R2, V = 512, 2048, 1024, 2048


def setup_inputs():
    s, t = mx_kscale(R1), mx_kscale(R2)
    ratio = np.exp(np.random.standard_normal((F, R1 + R2)))
    conf = (0.5 + np.random.random(R1 + R2)) * np.concatenate([s, t])
    rig = np.maximum(np.random.standard_normal((R1, V)), 0) / np.sqrt(R1) / s[:, None]
    roam = np.maximum(np.random.standard_normal((R2, V)), 0) / np.sqrt(R2) / t[:, None]
    rig_words, rig_scales = pack4(rig)
    return {"ratio": bf(ratio),
            "conf": bf(conf),
            "rig_words": rig_words,
            "rig_scales": rig_scales,
            "roam": bf(roam),
            "prior": bf(0.5 * np.random.standard_normal(V))}


def reference(ratio, conf, rig_words, rig_scales, roam, prior):
    e = np.log(f64(ratio)) * f64(conf)
    e_rig = mxq(e[:, :R1], 1, "e4m3")
    e_roam = mxq(e[:, R1:], 1, "e4m3")
    a = unpack4(rig_words, rig_scales)
    b = mxq(f64(roam), 0, "e4m3")
    z = (e_rig @ a) + (e_roam @ b) + f64(prior)
    occ = 1.0 / (1.0 + np.exp(z))
    return z, occ

@@ -1,0 +1,427 @@
+from contextlib import ExitStack
+
+import concourse.mybir as mybir
+from concourse.masks import make_identity
+
+F32 = mybir.dt.float32
+BF16 = mybir.dt.bfloat16
+I32 = mybir.dt.int32
+U32 = mybir.dt.uint32
+U8 = mybir.dt.uint8
+E4M3X4 = mybir.dt.float8_e4m3fn_x4
+E2M1X4 = mybir.dt.float4_e2m1fn_x4
+ACT = mybir.ActivationFunctionType
+ALU = mybir.AluOpType
+
+FRAMES, RIG, ROAM, VOX = 512, 2048, 1024, 2048
+FLOPS = 2 * FRAMES * (RIG + ROAM) * VOX
+P = 128
+NF = 4
+NN = 4
+NG = 6
+W = 512
+
+Z_BANKS = 6
+
+
+def tile_probabilistic_visual_hull_s1_kernel(
+    tc, ratio, conf, rig_words, rig_scales, roam, prior, out_0, out_1
+):
+    nc = tc.nc
+    with ExitStack() as ctx:
+        keep = ctx.enter_context(tc.tile_pool(name="keep", bufs=1))
+        work = ctx.enter_context(tc.tile_pool(name="work", bufs=3))
+        psum = ctx.enter_context(tc.psum_pool(name="psum", bufs=1))
+        ctx.enter_context(tc.manual_schedule())
+
+        ident = keep.tile([P, P], F32, name="ident")
+        make_identity(nc, ident[:])
+        rows = keep.tile([P, 512], BF16, name="rows")
+        nc.vector.memset(rows[:], 0.0)
+        warm = keep.tile([P, 2], F32, name="warm")
+        nc.vector.memset(warm[:, 0:1], 1.0)
+        nc.scalar.activation(out=warm[:, 1:2], in_=warm[:, 0:1], func=ACT.Ln)
+        planes = keep.tile([P, 4, VOX], U8, name="planes", align_bytes=64)
+        nc.vector.memset(planes[:].rearrange("p g n -> p (g n)").bitcast(I32), 0)
+
+        nc.sync.dma_start(out=rows[0:4, :], in_=conf[0:2048].rearrange("(g c) -> g c", g=4))
+        nc.sync.dma_start(out=rows[4:6, :], in_=conf[2048:3072].rearrange("(g c) -> g c", g=2))
+        nc.sync.dma_start(out=rows[8:12, :], in_=prior.rearrange("(r c) -> r c", r=4))
+
+        ratio_sb = [keep.tile([P, RIG + ROAM], BF16, name="ratio%d" % f, align_bytes=64) for f in range(NF)]
+        words_sb = keep.tile([P, 4, 2 * VOX], U8, name="words_sb", align_bytes=64)
+        raw = [[keep.tile([P, 4, 1024], BF16, name="raw%d_%d" % (g, h), align_bytes=64) for h in range(2)] for g in range(2)]
+
+        def load_ratio(f, gp0, gp1):
+            c = slice(1024 * gp0, 1024 * gp1)
+            nc.sync.dma_start(out=ratio_sb[f][:, c], in_=ratio[P * f : P * (f + 1), c])
+
+        def load_raw(g, n0, n1):
+            h = n0 // 2
+            c = slice(W * n0 - 1024 * h, W * n1 - 1024 * h)
+            nc.sync.dma_start(
+                out=raw[g][h][:, :, c],
+                in_=roam[512 * g : 512 * (g + 1), W * n0 : W * n1].rearrange("(p j) n -> p j n", j=4),
+            )
+
+        def load_words(n0, n1):
+            nc.sync.dma_start(
+                out=words_sb[:, :, 2 * W * n0 : 2 * W * n1].bitcast(I32),
+                in_=rig_words[:, :, 2 * W * n0 : 2 * W * n1].rearrange("g p b -> p g b").bitcast(I32),
+            )
+
+        def load_scales():
+            for q in range(4):
+                nc.sync.dma_start(
+                    out=planes[32 * q : 32 * q + 4, :, :].bitcast(I32),
+                    in_=rig_scales[:, 4 * q : 4 * q + 4, :].rearrange("g r n -> r g n").bitcast(I32),
+                )
+
+        e_codes = [keep.tile([P, NG, P], U32, name="ec%d" % f, align_bytes=64) for f in range(NF)]
+        e_scales = [keep.tile([P, NG, P], U8, name="es%d" % f, align_bytes=64) for f in range(NF)]
+        b_codes = [[keep.tile([P, W], U32, name="bc%d_%d" % (g, n), align_bytes=64) for n in range(NN)] for g in range(2)]
+        b_scales = [[keep.tile([P, W], U8, name="bs%d_%d" % (g, n), align_bytes=64) for n in range(NN)] for g in range(2)]
+        conf_sb = keep.tile([P, NG, 4], BF16, name="conf_sb")
+        prior_w = keep.tile([P, 4, 2], F32, name="prior_w")
+        prior_sb = keep.tile([P, VOX], BF16, name="prior_sb")
+
+        tfree = [0, 1]
+        tname = {}
+
+        def tbank():
+            return tfree.pop(0)
+
+        def consts_a():
+            cw = rows[:].bitcast(F32)
+            k = tbank()
+            ct = psum.tile([P, 2, P], F32, name="ct", tag="t%d" % k)
+            for u in range(2):
+                nc.tensor.transpose(ct[:, u, :], cw[:, u:256:2], ident[:])
+            nc.vector.tensor_copy(
+                out=conf_sb[:].rearrange("p g t -> p (g t)").bitcast(F32).rearrange("p (g u) -> p g u", u=2),
+                in_=ct[:, :, 0:6].rearrange("p u g -> p g u"),
+            )
+            nc.vector.tensor_copy(out=prior_w[:], in_=ct[:, :, 8:12].rearrange("p u r -> p r u"))
+            tfree.append(k)
+
+        def consts_b(h):
+            pt = psum.tile([P, 2, 2, P], F32, name="pt", tag="z%d" % (5 - h))
+            for r in range(2):
+                for u in range(2):
+                    nc.tensor.transpose(
+                        pt[:, r, u, :], prior_w[:, 2 * h + r, u : u + 1].to_broadcast([P, P]), ident[:]
+                    )
+            nc.vector.tensor_copy(
+                out=prior_sb[:, 1024 * h : 1024 * (h + 1)].bitcast(F32).rearrange("p (r q u) -> p r q u", r=2, u=2),
+                in_=pt[:].rearrange("p r u q -> p r q u"),
+            )
+
+        tb = {}
+        lnt = {}
+        eg = {}
+        bg = {}
+        zb = {}
+        zt = {}
+        free = list(range(Z_BANKS))
+        zbank = {}
+        done = {}
+
+        def T(f, gp):
+            k = tbank()
+            tname[f, gp] = k
+            xt = psum.tile([P, 2, 2, P], F32, name="xt", tag="t%d" % k)
+            w = ratio_sb[f][:].bitcast(F32)
+            for g in range(2):
+                for u in range(2):
+                    base = 256 * (2 * gp + g)
+                    nc.tensor.transpose(xt[:, u, g, :], w[:, base + u : base + 256 : 2], ident[:])
+            tb[f, gp] = xt
+
+        def L(f, gp):
+            ln = work.tile([P, 2, P, 4], F32, name="ln", bufs=6, align_bytes=64)
+            nc.scalar.activation(
+                out=ln[:].rearrange("p g r (u e) -> p (g r) u e", e=2),
+                in_=tb[f, gp][:].rearrange("p u g r -> p (u g r)").bitcast(BF16).rearrange("p (u x e) -> p x u e", u=2, e=2),
+                func=ACT.Ln,
+            )
+            lnt[f, gp] = ln
+            tfree.append(tname[f, gp])
+
+        def M(f, gp):
+            t = work.tile([P, 2, P, 4], BF16, name="eg", bufs=4, align_bytes=64)
+            nc.vector.tensor_tensor(
+                out=t[:],
+                in0=lnt[f, gp][:],
+                in1=conf_sb[:, 2 * gp : 2 * gp + 2, :].unsqueeze(2).to_broadcast([P, 2, P, 4]),
+                op=ALU.mult,
+            )
+            eg[f, gp] = t
+
+        def Q(f, gp):
+            nc.vector.quantize_mx(
+                out=e_codes[f][:, 2 * gp : 2 * gp + 2, :].rearrange("p g r -> p (g r)").bitcast(E4M3X4),
+                scales=e_scales[f][:, 2 * gp : 2 * gp + 2, :].rearrange("p g r -> p (g r)"),
+                in_=eg[f, gp][:].rearrange("p g r t -> p (g r t)"),
+            )
+
+        def BI(g, n, eng):
+            t = work.tile([P, W, 4], BF16, name="bg", bufs=5, align_bytes=64)
+            src = raw[g][n // 2][:, :, W * (n % 2) : W * (n % 2 + 1)].rearrange("p t c -> p c t")
+            dst = t[:].rearrange("p (c i) t -> p c t i", i=4)
+            src = src.rearrange("p (c i) t -> p c t i", i=4)
+            if eng == "V":
+                nc.vector.tensor_copy(out=dst, in_=src)
+            else:
+                nc.scalar.copy(out=dst, in_=src)
+            bg[g, n] = t
+
+        def BQ(g, n):
+            nc.vector.quantize_mx(
+                out=b_codes[g][n][:].bitcast(E4M3X4),
+                scales=b_scales[g][n][:],
+                in_=bg[g, n][:].rearrange("p c t -> p (c t)"),
+            )
+
+        def MM(f, n, gs):
+            for g in gs:
+                if (f, n) not in zb:
+                    k = free.pop(0)
+                    zbank[f, n] = k
+                    zb[f, n] = psum.tile([P, W], F32, name="acc", tag="z%d" % k)
+                    done[f, n] = 0
+                first = done[f, n] == 0
+                done[f, n] += 1
+                last = done[f, n] == NG
+                cols = slice(W * n, W * (n + 1))
+                if g < 4:
+                    rhs = words_sb[:, g, 2 * W * n : 2 * W * (n + 1)].bitcast(E2M1X4)
+                    rsc = planes[:, g, cols]
+                else:
+                    rhs = b_codes[g - 4][n][:].bitcast(E4M3X4)
+                    rsc = b_scales[g - 4][n][:]
+                nc.tensor.matmul_mx(
+                    out=zb[f, n][:],
+                    lhsT=e_codes[f][:, g, :].bitcast(E4M3X4),
+                    lhsT_scale=e_scales[f][:, g, :],
+                    rhs=rhs,
+                    rhs_scale=rsc,
+                    start=first,
+                    stop=last,
+                )
+
+        def ADD(f, n):
+            cols = slice(W * n, W * (n + 1))
+            z = work.tile([P, W], F32, name="z", bufs=11)
+            nc.vector.tensor_tensor(out=z[:], in0=zb[f, n][:], in1=prior_sb[:, cols], op=ALU.add)
+            free.append(zbank[f, n])
+            zt[f, n] = z
+            nc.sync.dma_start(out=out_0[P * f : P * (f + 1), cols], in_=z[:])
+
+        def SIG(f, n):
+            cols = slice(W * n, W * (n + 1))
+            o = work.tile([P, W], F32, name="o", bufs=11)
+            nc.scalar.activation(out=o[:], in_=zt[f, n][:], func=ACT.Sigmoid, scale=-1.0)
+            nc.sync.dma_start(out=out_1[P * f : P * (f + 1), cols], in_=o[:])
+
+        load_ratio(3, 0, 1)
+        load_ratio(3, 1, 2)
+        load_ratio(3, 2, 3)
+        load_ratio(2, 1, 2)
+        load_ratio(0, 0, 2)
+        load_scales()
+        load_words(0, 2)
+        load_ratio(2, 0, 1)
+        load_ratio(2, 2, 3)
+        load_raw(0, 0, 1)
+        load_ratio(1, 2, 3)
+        load_ratio(0, 2, 3)
+        load_ratio(1, 0, 1)
+        load_raw(1, 0, 2)
+        load_ratio(1, 1, 2)
+        load_raw(0, 1, 2)
+        load_raw(0, 2, 4)
+        load_words(2, 4)
+        load_raw(1, 2, 4)
+        consts_a()
+        T(3, 0)
+        consts_b(0)
+        consts_b(1)
+        T(3, 1)
+        L(3, 0)
+        L(3, 1)
+        T(2, 1)
+        M(3, 0)
+        L(2, 1)
+        T(0, 1)
+        M(3, 1)
+        L(0, 1)
+        T(3, 2)
+        M(2, 1)
+        L(3, 2)
+        Q(3, 0)
+        T(0, 0)
+        M(0, 1)
+        L(0, 0)
+        T(2, 0)
+        Q(3, 1)
+        Q(2, 1)
+        Q(0, 1)
+        L(2, 0)
+        T(2, 2)
+        M(0, 0)
+        MM(2, 1, [2])
+        MM(3, 0, [0])
+        L(2, 2)
+        M(3, 2)
+        MM(0, 0, [3])
+        MM(2, 1, [3])
+        MM(3, 1, [2, 1])
+        BI(0, 0, "S")
+        Q(0, 0)
+        T(1, 2)
+        M(2, 2)
+        T(0, 2)
+        M(2, 0)
+        MM(3, 0, [3])
+        MM(0, 1, [1])
+        L(0, 2)
+        MM(0, 1, [3])
+        MM(3, 1, [0])
+        Q(2, 2)
+        MM(0, 1, [0])
+        Q(2, 0)
+        MM(0, 0, [0])
+        L(1, 2)
+        MM(2, 0, [3])
+        M(0, 2)
+        MM(2, 1, [0])
+        MM(0, 0, [1])
+        MM(2, 0, [1])
+        BI(1, 0, "S")
+        BQ(0, 0)
+        MM(2, 0, [2])
+        MM(3, 1, [3])
+        MM(0, 1, [2])
+        Q(0, 2)
+        MM(2, 0, [0])
+        BI(1, 1, "V")
+        MM(0, 0, [2])
+        T(1, 1)
+        BI(0, 1, "S")
+        BQ(1, 0)
+        T(1, 0)
+        Q(3, 2)
+        MM(2, 0, [4])
+        BQ(1, 1)
+        MM(2, 0, [5])
+        MM(0, 0, [4])
+        ADD(2, 0)
+        MM(0, 0, [5])
+        L(1, 0)
+        MM(3, 0, [2])
+        ADD(0, 0)
+        MM(3, 0, [4, 5])
+        BQ(0, 1)
+        MM(3, 0, [1])
+        BI(0, 2, "S")
+        MM(3, 1, [5])
+        ADD(3, 0)
+        MM(2, 1, [5, 4])
+        M(1, 2)
+        MM(0, 1, [4])
+        MM(3, 1, [4])
+        MM(2, 1, [1])
+        MM(0, 1, [5])
+        L(1, 1)
+        ADD(2, 1)
+        MM(0, 2, [2, 0])
+        ADD(3, 1)
+        MM(0, 2, [1])
+        MM(2, 3, [3])
+        MM(2, 2, [0])
+        ADD(0, 1)
+        MM(3, 2, [1])
+        MM(2, 2, [3])
+        Q(1, 2)
+        MM(2, 3, [1])
+        BI(1, 2, "V")
+        MM(0, 2, [3])
+        MM(3, 2, [3])
+        SIG(3, 0)
+        MM(3, 2, [2, 0])
+        BQ(0, 2)
+        SIG(3, 1)
+        MM(1, 1, [5])
+        MM(2, 2, [1])
+        BQ(1, 2)
+        SIG(2, 0)
+        MM(3, 2, [4])
+        MM(2, 2, [4])
+        M(1, 0)
+        SIG(0, 0)
+        MM(3, 2, [5])
+        MM(2, 2, [2])
+        SIG(2, 1)
+        MM(0, 2, [5, 4])
+        ADD(3, 2)
+        SIG(0, 1)
+        MM(1, 0, [5])
+        MM(1, 1, [4])
+        Q(1, 0)
+        SIG(3, 2)
+        MM(2, 2, [5])
+        M(1, 1)
+        MM(2, 3, [0])
+        MM(1, 0, [4])
+        BI(1, 3, "S")
+        MM(1, 2, [4, 1])
+        ADD(2, 2)
+        MM(1, 1, [1])
+        MM(1, 2, [5])
+        Q(1, 1)
+        MM(1, 2, [0])
+        ADD(0, 2)
+        MM(2, 3, [2])
+        SIG(2, 2)
+        MM(1, 2, [2])
+        BI(0, 3, "V")
+        MM(1, 3, [1])
+        SIG(0, 2)
+        MM(1, 1, [0])
+        MM(1, 2, [3])
+        MM(1, 0, [3])
+        ADD(1, 2)
+        MM(1, 1, [2, 3])
+        BQ(0, 3)
+        MM(1, 3, [0])
+        SIG(1, 2)
+        MM(1, 0, [2])
+        ADD(1, 1)
+        MM(3, 3, [0])
+        MM(1, 0, [0])
+        BQ(1, 3)
+        MM(1, 0, [1])
+        SIG(1, 1)
+        MM(1, 3, [3])
+        MM(2, 3, [4])
+        ADD(1, 0)
+        MM(2, 3, [5])
+        MM(1, 3, [4])
+        ADD(2, 3)
+        SIG(1, 0)
+        MM(0, 3, [1, 4])
+        MM(1, 3, [2])
+        SIG(2, 3)
+        MM(1, 3, [5])
+        MM(0, 3, [5])
+        ADD(1, 3)
+        MM(3, 3, [3])
+        MM(0, 3, [2, 3])
+        SIG(1, 3)
+        MM(0, 3, [0])
+        MM(3, 3, [5])
+        ADD(0, 3)
+        MM(3, 3, [2, 1, 4])
+        SIG(0, 3)
+        ADD(3, 3)
+        SIG(3, 3)

@@ -49,26 +49,30 @@ def tile_probabilistic_visual_hull_s1_kernel(
         nc.sync.dma_start(out=rows[8:12, :], in_=prior.rearrange("(r c) -> r c", r=4))
 
         ratio_sb = [keep.tile([P, RIG + ROAM], BF16, name="ratio%d" % f, align_bytes=64) for f in range(NF)]
-        words_sb = keep.tile([P, 4, 2 * VOX], U8, name="words_sb", align_bytes=64)
-        raw = [[keep.tile([P, 4, 1024], BF16, name="raw%d_%d" % (g, h), align_bytes=64) for h in range(2)] for g in range(2)]
+        words = {}
+        raw = {}
 
         def load_ratio(f, gp0, gp1):
             c = slice(1024 * gp0, 1024 * gp1)
             nc.sync.dma_start(out=ratio_sb[f][:, c], in_=ratio[P * f : P * (f + 1), c])
 
         def load_raw(g, n0, n1):
-            h = n0 // 2
-            c = slice(W * n0 - 1024 * h, W * n1 - 1024 * h)
+            t = keep.tile([P, 4, W * (n1 - n0)], BF16, name="raw%d_%d" % (g, n0), align_bytes=64)
             nc.sync.dma_start(
-                out=raw[g][h][:, :, c],
+                out=t[:],
                 in_=roam[512 * g : 512 * (g + 1), W * n0 : W * n1].rearrange("(p j) n -> p j n", j=4),
             )
+            for n in range(n0, n1):
+                raw[g, n] = t[:, :, W * (n - n0) : W * (n - n0 + 1)]
 
         def load_words(n0, n1):
+            t = keep.tile([P, 4, 2 * W * (n1 - n0)], U8, name="words%d" % n0, align_bytes=64)
             nc.sync.dma_start(
-                out=words_sb[:, :, 2 * W * n0 : 2 * W * n1].bitcast(I32),
+                out=t[:].bitcast(I32),
                 in_=rig_words[:, :, 2 * W * n0 : 2 * W * n1].rearrange("g p b -> p g b").bitcast(I32),
             )
+            for n in range(n0, n1):
+                words[n] = t[:, :, 2 * W * (n - n0) : 2 * W * (n - n0 + 1)]
 
         def load_scales():
             for q in range(4):
@@ -166,9 +170,9 @@ def tile_probabilistic_visual_hull_s1_kernel(
 
         def BI(g, n, eng):
             t = work.tile([P, W, 4], BF16, name="bg", bufs=5, align_bytes=64)
-            src = raw[g][n // 2][:, :, W * (n % 2) : W * (n % 2 + 1)].rearrange("p t c -> p c t")
+            src = raw[g, n]
             dst = t[:].rearrange("p (c i) t -> p c t i", i=4)
-            src = src.rearrange("p (c i) t -> p c t i", i=4)
+            src = src.rearrange("p t (c i) -> p c t i", i=4)
             if eng == "V":
                 nc.vector.tensor_copy(out=dst, in_=src)
             else:
@@ -194,7 +198,7 @@ def tile_probabilistic_visual_hull_s1_kernel(
                 last = done[f, n] == NG
                 cols = slice(W * n, W * (n + 1))
                 if g < 4:
-                    rhs = words_sb[:, g, 2 * W * n : 2 * W * (n + 1)].bitcast(E2M1X4)
+                    rhs = words[n][:, g, :].bitcast(E2M1X4)
                     rsc = planes[:, g, cols]
                 else:
                     rhs = b_codes[g - 4][n][:].bitcast(E4M3X4)

@@ -35,25 +35,25 @@ def tile_probabilistic_visual_hull_s1_kernel(
         ctx.enter_context(tc.manual_schedule())
 
         ident = keep.tile([P, P], F32, name="ident")
-        make_identity(nc, ident[:])
         rows = keep.tile([P, 512], BF16, name="rows")
-        nc.vector.memset(rows[:], 0.0)
+        nc.gpsimd.memset(rows[:].bitcast(F32), 0.0)
+        make_identity(nc, ident[:])
+        nc.scalar.dma_start(out=rows[0:4, :], in_=conf[0:2048].rearrange("(g c) -> g c", g=4))
+        nc.scalar.dma_start(out=rows[4:6, :], in_=conf[2048:3072].rearrange("(g c) -> g c", g=2))
+        nc.scalar.dma_start(out=rows[8:12, :], in_=prior.rearrange("(r c) -> r c", r=4))
         warm = keep.tile([P, 2], F32, name="warm")
         nc.vector.memset(warm[:, 0:1], 1.0)
         nc.scalar.activation(out=warm[:, 1:2], in_=warm[:, 0:1], func=ACT.Ln)
-        planes = keep.tile([P, 4, VOX], U8, name="planes", align_bytes=64)
-        nc.vector.memset(planes[:].rearrange("p g n -> p (g n)").bitcast(I32), 0)
-
-        nc.sync.dma_start(out=rows[0:4, :], in_=conf[0:2048].rearrange("(g c) -> g c", g=4))
-        nc.sync.dma_start(out=rows[4:6, :], in_=conf[2048:3072].rearrange("(g c) -> g c", g=2))
-        nc.sync.dma_start(out=rows[8:12, :], in_=prior.rearrange("(r c) -> r c", r=4))
+        planes = [keep.tile([P, 4, 1024], U8, name="planes%d" % h, align_bytes=64) for h in range(2)]
+        for h in range(2):
+            nc.vector.memset(planes[h][:].rearrange("p g n -> p (g n)").bitcast(I32), 0)
 
         ratio_sb = [keep.tile([P, RIG + ROAM], BF16, name="ratio%d" % f, align_bytes=64) for f in range(NF)]
         words = {}
         raw = {}
 
-        def load_ratio(f, gp0, gp1):
-            c = slice(1024 * gp0, 1024 * gp1)
+        def load_ratio(f, g0, g1):
+            c = slice(512 * g0, 512 * g1)
             nc.sync.dma_start(out=ratio_sb[f][:, c], in_=ratio[P * f : P * (f + 1), c])
 
         def load_raw(g, n0, n1):
@@ -74,11 +74,11 @@ def tile_probabilistic_visual_hull_s1_kernel(
             for n in range(n0, n1):
                 words[n] = t[:, :, 2 * W * (n - n0) : 2 * W * (n - n0 + 1)]
 
-        def load_scales():
-            for q in range(4):
+        def load_scales(h):
+            for r in range(4):
                 nc.sync.dma_start(
-                    out=planes[32 * q : 32 * q + 4, :, :].bitcast(I32),
-                    in_=rig_scales[:, 4 * q : 4 * q + 4, :].rearrange("g r n -> r g n").bitcast(I32),
+                    out=planes[h][r:P:32, :, :].bitcast(I32),
+                    in_=rig_scales[:, r:16:4, 1024 * h : 1024 * (h + 1)].rearrange("g q n -> q g n").bitcast(I32),
                 )
 
         e_codes = [keep.tile([P, NG, P], U32, name="ec%d" % f, align_bytes=64) for f in range(NF)]
@@ -97,8 +97,7 @@ def tile_probabilistic_visual_hull_s1_kernel(
 
         def consts_a():
             cw = rows[:].bitcast(F32)
-            k = tbank()
-            ct = psum.tile([P, 2, P], F32, name="ct", tag="t%d" % k)
+            ct = psum.tile([P, 2, P], F32, name="ct", tag="z3")
             for u in range(2):
                 nc.tensor.transpose(ct[:, u, :], cw[:, u:256:2], ident[:])
             nc.vector.tensor_copy(
@@ -106,7 +105,6 @@ def tile_probabilistic_visual_hull_s1_kernel(
                 in_=ct[:, :, 0:6].rearrange("p u g -> p g u"),
             )
             nc.vector.tensor_copy(out=prior_w[:], in_=ct[:, :, 8:12].rearrange("p u r -> p r u"))
-            tfree.append(k)
 
         def consts_b(h):
             pt = psum.tile([P, 2, 2, P], F32, name="pt", tag="z%d" % (5 - h))
@@ -125,41 +123,41 @@ def tile_probabilistic_visual_hull_s1_kernel(
         eg = {}
         bg = {}
         zb = {}
-        zt = {}
         free = list(range(Z_BANKS))
         zbank = {}
         done = {}
 
-        def T(f, gp):
+        def T(f, g0, ng=2):
             k = tbank()
-            tname[f, gp] = k
-            xt = psum.tile([P, 2, 2, P], F32, name="xt", tag="t%d" % k)
+            tname[f, g0] = k
+            xt = psum.tile([P, 2, ng, P], F32, name="xt", tag="t%d" % k)
             w = ratio_sb[f][:].bitcast(F32)
-            for g in range(2):
+            for g in range(ng):
                 for u in range(2):
-                    base = 256 * (2 * gp + g)
+                    base = 256 * (g0 + g)
                     nc.tensor.transpose(xt[:, u, g, :], w[:, base + u : base + 256 : 2], ident[:])
-            tb[f, gp] = xt
+            tb[f, g0] = xt
 
-        def L(f, gp):
-            ln = work.tile([P, 2, P, 4], F32, name="ln", bufs=6, align_bytes=64)
+        def L(f, g0, ng=2):
+            ln = work.tile([P, ng, P, 4], F32, name="ln", bufs=6, align_bytes=64)
             nc.scalar.activation(
                 out=ln[:].rearrange("p g r (u e) -> p (g r) u e", e=2),
-                in_=tb[f, gp][:].rearrange("p u g r -> p (u g r)").bitcast(BF16).rearrange("p (u x e) -> p x u e", u=2, e=2),
+                in_=tb[f, g0][:].rearrange("p u g r -> p (u g r)").bitcast(BF16).rearrange("p (u x e) -> p x u e", u=2, e=2),
                 func=ACT.Ln,
             )
-            lnt[f, gp] = ln
-            tfree.append(tname[f, gp])
+            lnt[f, g0] = ln
+            tfree.append(tname[f, g0])
 
-        def M(f, gp):
-            t = work.tile([P, 2, P, 4], BF16, name="eg", bufs=4, align_bytes=64)
+        def M(f, g0, ng=2):
+            gp = g0 // 2
+            if (f, gp) not in eg:
+                eg[f, gp] = work.tile([P, 2, P, 4], BF16, name="eg", bufs=6, align_bytes=64)
             nc.vector.tensor_tensor(
-                out=t[:],
-                in0=lnt[f, gp][:],
-                in1=conf_sb[:, 2 * gp : 2 * gp + 2, :].unsqueeze(2).to_broadcast([P, 2, P, 4]),
+                out=eg[f, gp][:, g0 % 2 : g0 % 2 + ng],
+                in0=lnt[f, g0][:],
+                in1=conf_sb[:, g0 : g0 + ng, :].unsqueeze(2).to_broadcast([P, ng, P, 4]),
                 op=ALU.mult,
             )
-            eg[f, gp] = t
 
         def Q(f, gp):
             nc.vector.quantize_mx(
@@ -169,7 +167,7 @@ def tile_probabilistic_visual_hull_s1_kernel(
             )
 
         def BI(g, n, eng):
-            t = work.tile([P, W, 4], BF16, name="bg", bufs=5, align_bytes=64)
+            t = work.tile([P, W, 4], BF16, name="bg", bufs=4, align_bytes=64)
             src = raw[g, n]
             dst = t[:].rearrange("p (c i) t -> p c t i", i=4)
             src = src.rearrange("p t (c i) -> p c t i", i=4)
@@ -199,7 +197,7 @@ def tile_probabilistic_visual_hull_s1_kernel(
                 cols = slice(W * n, W * (n + 1))
                 if g < 4:
                     rhs = words[n][:, g, :].bitcast(E2M1X4)
-                    rsc = planes[:, g, cols]
+                    rsc = planes[n // 2][:, g, W * (n % 2) : W * (n % 2 + 1)]
                 else:
                     rhs = b_codes[g - 4][n][:].bitcast(E4M3X4)
                     rsc = b_scales[g - 4][n][:]
@@ -213,219 +211,258 @@ def tile_probabilistic_visual_hull_s1_kernel(
                     stop=last,
                 )
 
+        zt = {}
+        ot = {}
+        half_done = {}
+
+        def out_tile(tiles, f, n, kind):
+            h = n // 2
+            if (f, h) not in tiles:
+                tiles[f, h] = keep.tile([P, 2 * W], F32, name="%s%d_%d" % (kind, f, h))
+            return tiles[f, h]
+
+        def store(tiles, dst, f, n, kind):
+            h = n // 2
+            k = (kind, f, h)
+            half_done[k] = half_done.get(k, 0) + 1
+            if (f, h) in SINGLE:
+                nc.sync.dma_start(
+                    out=dst[P * f : P * (f + 1), W * n : W * (n + 1)],
+                    in_=tiles[f, h][:, W * (n % 2) : W * (n % 2 + 1)],
+                )
+            elif half_done[k] == 2:
+                nc.sync.dma_start(
+                    out=dst[P * f : P * (f + 1), 2 * W * h : 2 * W * (h + 1)], in_=tiles[f, h][:]
+                )
+
         def ADD(f, n):
-            cols = slice(W * n, W * (n + 1))
-            z = work.tile([P, W], F32, name="z", bufs=11)
-            nc.vector.tensor_tensor(out=z[:], in0=zb[f, n][:], in1=prior_sb[:, cols], op=ALU.add)
+            z = out_tile(zt, f, n, "z")
+            nc.vector.tensor_tensor(
+                out=z[:, W * (n % 2) : W * (n % 2 + 1)],
+                in0=zb[f, n][:],
+                in1=prior_sb[:, W * n : W * (n + 1)],
+                op=ALU.add,
+            )
             free.append(zbank[f, n])
-            zt[f, n] = z
-            nc.sync.dma_start(out=out_0[P * f : P * (f + 1), cols], in_=z[:])
+            store(zt, out_0, f, n, "z")
 
         def SIG(f, n):
-            cols = slice(W * n, W * (n + 1))
-            o = work.tile([P, W], F32, name="o", bufs=11)
-            nc.scalar.activation(out=o[:], in_=zt[f, n][:], func=ACT.Sigmoid, scale=-1.0)
-            nc.sync.dma_start(out=out_1[P * f : P * (f + 1), cols], in_=o[:])
+            o = out_tile(ot, f, n, "o")
+            nc.scalar.activation(
+                out=o[:, W * (n % 2) : W * (n % 2 + 1)],
+                in_=zt[f, n // 2][:, W * (n % 2) : W * (n % 2 + 1)],
+                func=ACT.Sigmoid,
+                scale=-1.0,
+            )
+            store(ot, out_1, f, n, "o")
 
+        SINGLE = {(1, 0), (2, 0), (3, 0), (0, 0)}
         load_ratio(3, 0, 1)
         load_ratio(3, 1, 2)
-        load_ratio(3, 2, 3)
-        load_ratio(2, 1, 2)
-        load_ratio(0, 0, 2)
-        load_scales()
-        load_words(0, 2)
-        load_ratio(2, 0, 1)
-        load_ratio(2, 2, 3)
-        load_raw(0, 0, 1)
-        load_ratio(1, 2, 3)
-        load_ratio(0, 2, 3)
-        load_ratio(1, 0, 1)
-        load_raw(1, 0, 2)
-        load_ratio(1, 1, 2)
-        load_raw(0, 1, 2)
-        load_raw(0, 2, 4)
+        load_ratio(3, 2, 4)
+        load_ratio(1, 0, 4)
+        load_ratio(2, 0, 2)
+        load_ratio(1, 4, 6)
+        load_ratio(3, 4, 6)
+        load_ratio(0, 2, 4)
+        load_scales(1)
+        load_ratio(2, 2, 6)
         load_words(2, 4)
+        load_raw(0, 2, 4)
         load_raw(1, 2, 4)
+        load_ratio(0, 4, 6)
+        load_ratio(0, 0, 2)
+        load_raw(0, 1, 2)
+        load_raw(1, 0, 2)
+        load_scales(0)
+        load_words(0, 2)
+        load_raw(0, 0, 1)
+        T(3, 0, 1)
         consts_a()
-        T(3, 0)
+        T(3, 1, 1)
         consts_b(0)
         consts_b(1)
-        T(3, 1)
-        L(3, 0)
-        L(3, 1)
-        T(2, 1)
-        M(3, 0)
-        L(2, 1)
-        T(0, 1)
-        M(3, 1)
-        L(0, 1)
+        L(3, 0, 1)
+        L(3, 1, 1)
         T(3, 2)
-        M(2, 1)
+        M(3, 0, 1)
+        M(3, 1, 1)
         L(3, 2)
-        Q(3, 0)
-        T(0, 0)
-        M(0, 1)
-        L(0, 0)
-        T(2, 0)
-        Q(3, 1)
-        Q(2, 1)
-        Q(0, 1)
-        L(2, 0)
-        T(2, 2)
-        M(0, 0)
-        MM(2, 1, [2])
-        MM(3, 0, [0])
-        L(2, 2)
-        M(3, 2)
-        MM(0, 0, [3])
-        MM(2, 1, [3])
-        MM(3, 1, [2, 1])
-        BI(0, 0, "S")
-        Q(0, 0)
         T(1, 2)
-        M(2, 2)
+        Q(3, 0)
+        L(1, 2)
+        T(2, 0)
+        M(3, 2)
+        L(2, 0)
+        T(3, 4)
+        M(1, 2)
+        L(3, 4)
+        Q(3, 1)
         T(0, 2)
         M(2, 0)
-        MM(3, 0, [3])
-        MM(0, 1, [1])
         L(0, 2)
-        MM(0, 1, [3])
-        MM(3, 1, [0])
-        Q(2, 2)
-        MM(0, 1, [0])
-        Q(2, 0)
-        MM(0, 0, [0])
-        L(1, 2)
-        MM(2, 0, [3])
-        M(0, 2)
-        MM(2, 1, [0])
-        MM(0, 0, [1])
-        MM(2, 0, [1])
-        BI(1, 0, "S")
-        BQ(0, 0)
-        MM(2, 0, [2])
-        MM(3, 1, [3])
-        MM(0, 1, [2])
-        Q(0, 2)
-        MM(2, 0, [0])
-        BI(1, 1, "V")
-        MM(0, 0, [2])
-        T(1, 1)
-        BI(0, 1, "S")
-        BQ(1, 0)
-        T(1, 0)
-        Q(3, 2)
-        MM(2, 0, [4])
-        BQ(1, 1)
-        MM(2, 0, [5])
-        MM(0, 0, [4])
-        ADD(2, 0)
-        MM(0, 0, [5])
-        L(1, 0)
-        MM(3, 0, [2])
-        ADD(0, 0)
-        MM(3, 0, [4, 5])
-        BQ(0, 1)
-        MM(3, 0, [1])
-        BI(0, 2, "S")
-        MM(3, 1, [5])
-        ADD(3, 0)
-        MM(2, 1, [5, 4])
-        M(1, 2)
-        MM(0, 1, [4])
-        MM(3, 1, [4])
-        MM(2, 1, [1])
-        MM(0, 1, [5])
-        L(1, 1)
-        ADD(2, 1)
-        MM(0, 2, [2, 0])
-        ADD(3, 1)
-        MM(0, 2, [1])
-        MM(2, 3, [3])
-        MM(2, 2, [0])
-        ADD(0, 1)
-        MM(3, 2, [1])
-        MM(2, 2, [3])
-        Q(1, 2)
-        MM(2, 3, [1])
-        BI(1, 2, "V")
-        MM(0, 2, [3])
-        MM(3, 2, [3])
-        SIG(3, 0)
-        MM(3, 2, [2, 0])
-        BQ(0, 2)
-        SIG(3, 1)
-        MM(1, 1, [5])
-        MM(2, 2, [1])
-        BQ(1, 2)
-        SIG(2, 0)
-        MM(3, 2, [4])
-        MM(2, 2, [4])
-        M(1, 0)
-        SIG(0, 0)
-        MM(3, 2, [5])
-        MM(2, 2, [2])
-        SIG(2, 1)
-        MM(0, 2, [5, 4])
-        ADD(3, 2)
-        SIG(0, 1)
-        MM(1, 0, [5])
-        MM(1, 1, [4])
-        Q(1, 0)
-        SIG(3, 2)
-        MM(2, 2, [5])
-        M(1, 1)
-        MM(2, 3, [0])
-        MM(1, 0, [4])
-        BI(1, 3, "S")
-        MM(1, 2, [4, 1])
-        ADD(2, 2)
-        MM(1, 1, [1])
-        MM(1, 2, [5])
+        T(1, 4)
         Q(1, 1)
-        MM(1, 2, [0])
-        ADD(0, 2)
-        MM(2, 3, [2])
-        SIG(2, 2)
-        MM(1, 2, [2])
-        BI(0, 3, "V")
-        MM(1, 3, [1])
-        SIG(0, 2)
-        MM(1, 1, [0])
-        MM(1, 2, [3])
-        MM(1, 0, [3])
-        ADD(1, 2)
-        MM(1, 1, [2, 3])
-        BQ(0, 3)
-        MM(1, 3, [0])
-        SIG(1, 2)
-        MM(1, 0, [2])
-        ADD(1, 1)
-        MM(3, 3, [0])
-        MM(1, 0, [0])
-        BQ(1, 3)
-        MM(1, 0, [1])
-        SIG(1, 1)
+        Q(2, 0)
+        M(3, 4)
+        L(1, 4)
+        T(1, 0)
+        M(0, 2)
+        L(1, 0)
+        T(2, 2)
+        Q(3, 2)
+        L(2, 2)
+        M(1, 4)
+        T(2, 4)
+        MM(2, 3, [0])
+        MM(3, 3, [2])
+        L(2, 4)
+        M(1, 0)
+        MM(3, 2, [0])
+        MM(2, 2, [0])
         MM(1, 3, [3])
-        MM(2, 3, [4])
-        ADD(1, 0)
-        MM(2, 3, [5])
-        MM(1, 3, [4])
-        ADD(2, 3)
-        SIG(1, 0)
-        MM(0, 3, [1, 4])
-        MM(1, 3, [2])
-        SIG(2, 3)
-        MM(1, 3, [5])
-        MM(0, 3, [5])
-        ADD(1, 3)
         MM(3, 3, [3])
-        MM(0, 3, [2, 3])
-        SIG(1, 3)
-        MM(0, 3, [0])
+        Q(1, 2)
+        BI(0, 3, "S")
+        MM(1, 2, [2])
+        Q(1, 0)
+        MM(3, 3, [1])
+        M(2, 2)
+        MM(1, 3, [0])
+        MM(3, 2, [2])
+        MM(1, 3, [1])
+        MM(3, 2, [3])
+        M(2, 4)
+        MM(1, 3, [2])
+        MM(3, 2, [1])
+        MM(1, 2, [3])
+        BI(1, 3, "S")
+        MM(3, 3, [0])
+        Q(2, 1)
+        BI(1, 2, "V")
+        T(0, 4)
+        T(0, 0)
+        BQ(0, 3)
+        MM(2, 3, [3])
+        Q(2, 2)
+        BI(0, 2, "S")
+        MM(1, 3, [4])
+        BQ(1, 2)
+        MM(2, 2, [2])
+        MM(3, 3, [4])
+        BQ(1, 3)
+        MM(1, 2, [0])
+        MM(2, 3, [2])
+        BI(0, 1, "V")
+        MM(3, 2, [5])
         MM(3, 3, [5])
-        ADD(0, 3)
-        MM(3, 3, [2, 1, 4])
-        SIG(0, 3)
+        MM(1, 2, [1])
+        MM(2, 2, [1])
+        L(0, 0)
+        MM(1, 3, [5])
+        BQ(0, 2)
+        MM(2, 2, [3])
+        MM(2, 3, [5])
         ADD(3, 3)
+        MM(2, 3, [1])
+        BI(1, 1, "S")
+        MM(2, 3, [4])
+        BQ(0, 1)
+        MM(2, 2, [5])
+        MM(3, 2, [4])
+        ADD(2, 3)
+        MM(2, 2, [4])
+        MM(2, 1, [4])
+        ADD(3, 2)
+        MM(1, 2, [4, 5])
+        ADD(2, 2)
+        MM(1, 1, [4])
+        MM(3, 1, [4])
+        L(0, 4)
+        ADD(1, 2)
+        MM(1, 1, [0])
+        MM(2, 1, [1])
+        BQ(1, 1)
+        MM(2, 1, [3, 2])
+        ADD(1, 3)
+        MM(2, 1, [0, 5])
+        Q(0, 1)
+        MM(1, 1, [2])
+        ADD(2, 1)
+        MM(3, 1, [0])
+        MM(1, 1, [5])
+        M(0, 4)
+        MM(3, 1, [2])
+        SIG(1, 2)
+        MM(1, 0, [0])
+        MM(0, 3, [2])
+        SIG(1, 3)
+        MM(0, 2, [2])
+        M(0, 0)
+        MM(3, 1, [3])
         SIG(3, 3)
+        MM(1, 1, [1, 3])
+        SIG(3, 2)
+        MM(3, 1, [1])
+        Q(0, 2)
+        MM(0, 3, [3])
+        SIG(2, 1)
+        Q(0, 0)
+        MM(3, 1, [5])
+        MM(0, 1, [5])
+        SIG(2, 2)
+        ADD(3, 1)
+        MM(0, 2, [5])
+        MM(0, 1, [4])
+        SIG(2, 3)
+        ADD(1, 1)
+        MM(0, 2, [4])
+        MM(0, 1, [3])
+        SIG(3, 1)
+        BI(0, 0, "V")
+        MM(0, 1, [1])
+        MM(0, 2, [0])
+        BI(1, 0, "S")
+        MM(0, 1, [0, 2])
+        MM(0, 2, [3])
+        ADD(0, 1)
+        MM(0, 2, [1])
+        MM(0, 3, [1])
+        BQ(0, 0)
+        MM(0, 3, [0, 5])
+        ADD(0, 2)
+        MM(0, 3, [4])
+        MM(1, 0, [2])
+        SIG(0, 1)
+        ADD(0, 3)
+        MM(1, 0, [4])
+        MM(0, 0, [1])
+        SIG(0, 2)
+        BQ(1, 0)
+        MM(2, 0, [0])
+        MM(1, 0, [3])
+        SIG(0, 3)
+        MM(1, 0, [1])
+        MM(0, 0, [4])
+        SIG(1, 1)
+        MM(2, 0, [3])
+        MM(1, 0, [5])
+        MM(2, 0, [1])
+        ADD(1, 0)
+        MM(0, 0, [3])
+        MM(2, 0, [5])
+        MM(0, 0, [5])
+        SIG(1, 0)
+        MM(2, 0, [2, 4])
+        MM(0, 0, [2])
+        ADD(2, 0)
+        MM(0, 0, [0])
+        MM(3, 0, [5])
+        ADD(0, 0)
+        MM(3, 0, [2])
+        SIG(2, 0)
+        MM(3, 0, [1, 0])
+        SIG(0, 0)
+        MM(3, 0, [4, 3])
+        ADD(3, 0)
+        SIG(3, 0)

@@ -83,8 +83,8 @@ def tile_probabilistic_visual_hull_s1_kernel(
 
         e_codes = [keep.tile([P, NG, P], U32, name="ec%d" % f, align_bytes=64) for f in range(NF)]
         e_scales = [keep.tile([P, NG, P], U8, name="es%d" % f, align_bytes=64) for f in range(NF)]
-        b_codes = [[keep.tile([P, W], U32, name="bc%d_%d" % (g, n), align_bytes=64) for n in range(NN)] for g in range(2)]
-        b_scales = [[keep.tile([P, W], U8, name="bs%d_%d" % (g, n), align_bytes=64) for n in range(NN)] for g in range(2)]
+        b_codes = [keep.tile([P, 2, W], U32, name="bc%d" % n, align_bytes=64) for n in range(NN)]
+        b_scales = [keep.tile([P, 2, W], U8, name="bs%d" % n, align_bytes=64) for n in range(NN)]
         conf_sb = keep.tile([P, NG, 4], BF16, name="conf_sb")
         prior_w = keep.tile([P, 4, 2], F32, name="prior_w")
         prior_sb = keep.tile([P, VOX], BF16, name="prior_sb")
@@ -106,6 +106,8 @@ def tile_probabilistic_visual_hull_s1_kernel(
             )
             nc.vector.tensor_copy(out=prior_w[:], in_=ct[:, :, 8:12].rearrange("p u r -> p r u"))
 
+        pts = []
+
         def consts_b(h):
             pt = psum.tile([P, 2, 2, P], F32, name="pt", tag="z%d" % (5 - h))
             for r in range(2):
@@ -113,10 +115,16 @@ def tile_probabilistic_visual_hull_s1_kernel(
                     nc.tensor.transpose(
                         pt[:, r, u, :], prior_w[:, 2 * h + r, u : u + 1].to_broadcast([P, P]), ident[:]
                     )
-            nc.vector.tensor_copy(
-                out=prior_sb[:, 1024 * h : 1024 * (h + 1)].bitcast(F32).rearrange("p (r q u) -> p r q u", r=2, u=2),
-                in_=pt[:].rearrange("p r u q -> p r q u"),
-            )
+            pts.append(pt)
+
+        def XC(eng):
+            for h in range(2):
+                dst = prior_sb[:, 1024 * h : 1024 * (h + 1)].bitcast(F32).rearrange("p (r q u) -> p r q u", r=2, u=2)
+                src = pts[h][:].rearrange("p r u q -> p r q u")
+                if eng == "V":
+                    nc.vector.tensor_copy(out=dst, in_=src)
+                else:
+                    nc.scalar.copy(out=dst, in_=src)
 
         tb = {}
         lnt = {}
@@ -167,21 +175,20 @@ def tile_probabilistic_visual_hull_s1_kernel(
             )
 
         def BI(g, n, eng):
-            t = work.tile([P, W, 4], BF16, name="bg", bufs=4, align_bytes=64)
-            src = raw[g, n]
-            dst = t[:].rearrange("p (c i) t -> p c t i", i=4)
-            src = src.rearrange("p t (c i) -> p c t i", i=4)
+            if n not in bg:
+                bg[n] = work.tile([P, 2, W, 4], BF16, name="bg", bufs=3, align_bytes=64)
+            dst = bg[n][:, g].rearrange("p (c i) t -> p c t i", i=4)
+            src = raw[g, n].rearrange("p t (c i) -> p c t i", i=4)
             if eng == "V":
                 nc.vector.tensor_copy(out=dst, in_=src)
             else:
                 nc.scalar.copy(out=dst, in_=src)
-            bg[g, n] = t
 
-        def BQ(g, n):
+        def BQ(n):
             nc.vector.quantize_mx(
-                out=b_codes[g][n][:].bitcast(E4M3X4),
-                scales=b_scales[g][n][:],
-                in_=bg[g, n][:].rearrange("p c t -> p (c t)"),
+                out=b_codes[n][:].rearrange("p g c -> p (g c)").bitcast(E4M3X4),
+                scales=b_scales[n][:].rearrange("p g c -> p (g c)"),
+                in_=bg[n][:].rearrange("p g c t -> p (g c t)"),
             )
 
         def MM(f, n, gs):
@@ -199,8 +206,8 @@ def tile_probabilistic_visual_hull_s1_kernel(
                     rhs = words[n][:, g, :].bitcast(E2M1X4)
                     rsc = planes[n // 2][:, g, W * (n % 2) : W * (n % 2 + 1)]
                 else:
-                    rhs = b_codes[g - 4][n][:].bitcast(E4M3X4)
-                    rsc = b_scales[g - 4][n][:]
+                    rhs = b_codes[n][:, g - 4, :].bitcast(E4M3X4)
+                    rsc = b_scales[n][:, g - 4, :]
                 nc.tensor.matmul_mx(
                     out=zb[f, n][:],
                     lhsT=e_codes[f][:, g, :].bitcast(E4M3X4),
@@ -218,7 +225,7 @@ def tile_probabilistic_visual_hull_s1_kernel(
         def out_tile(tiles, f, n, kind):
             h = n // 2
             if (f, h) not in tiles:
-                tiles[f, h] = keep.tile([P, 2 * W], F32, name="%s%d_%d" % (kind, f, h))
+                tiles[f, h] = work.tile([P, 2 * W], F32, name=kind, bufs=6)
             return tiles[f, h]
 
         def store(tiles, dst, f, n, kind):
@@ -256,213 +263,206 @@ def tile_probabilistic_visual_hull_s1_kernel(
             )
             store(ot, out_1, f, n, "o")
 
-        SINGLE = {(1, 0), (2, 0), (3, 0), (0, 0)}
+        SINGLE = {(1, 0), (3, 0)}
         load_ratio(3, 0, 1)
         load_ratio(3, 1, 2)
-        load_ratio(3, 2, 4)
-        load_ratio(1, 0, 4)
-        load_ratio(2, 0, 2)
-        load_ratio(1, 4, 6)
-        load_ratio(3, 4, 6)
         load_ratio(0, 2, 4)
-        load_scales(1)
-        load_ratio(2, 2, 6)
-        load_words(2, 4)
-        load_raw(0, 2, 4)
-        load_raw(1, 2, 4)
-        load_ratio(0, 4, 6)
+        load_raw(0, 3, 4)
+        load_ratio(3, 2, 4)
         load_ratio(0, 0, 2)
-        load_raw(0, 1, 2)
-        load_raw(1, 0, 2)
+        load_ratio(3, 4, 6)
+        load_ratio(0, 4, 6)
+        load_ratio(2, 0, 6)
+        load_scales(1)
+        load_words(2, 4)
+        load_raw(1, 3, 4)
+        load_ratio(1, 0, 4)
+        load_raw(0, 1, 3)
+        load_raw(1, 2, 3)
+        load_ratio(1, 4, 6)
+        load_raw(1, 1, 2)
         load_scales(0)
         load_words(0, 2)
         load_raw(0, 0, 1)
+        load_raw(1, 0, 1)
         T(3, 0, 1)
         consts_a()
         T(3, 1, 1)
-        consts_b(0)
-        consts_b(1)
         L(3, 0, 1)
         L(3, 1, 1)
-        T(3, 2)
+        T(0, 2)
         M(3, 0, 1)
         M(3, 1, 1)
-        L(3, 2)
-        T(1, 2)
-        Q(3, 0)
-        L(1, 2)
-        T(2, 0)
-        M(3, 2)
-        L(2, 0)
-        T(3, 4)
-        M(1, 2)
-        L(3, 4)
-        Q(3, 1)
-        T(0, 2)
-        M(2, 0)
         L(0, 2)
-        T(1, 4)
-        Q(1, 1)
-        Q(2, 0)
-        M(3, 4)
-        L(1, 4)
-        T(1, 0)
+        BI(0, 3, "V")
+        consts_b(0)
+        consts_b(1)
+        T(3, 2)
+        XC("S")
         M(0, 2)
-        L(1, 0)
-        T(2, 2)
-        Q(3, 2)
-        L(2, 2)
-        M(1, 4)
-        T(2, 4)
-        MM(2, 3, [0])
-        MM(3, 3, [2])
-        L(2, 4)
-        M(1, 0)
-        MM(3, 2, [0])
-        MM(2, 2, [0])
-        MM(1, 3, [3])
-        MM(3, 3, [3])
-        Q(1, 2)
-        BI(0, 3, "S")
-        MM(1, 2, [2])
-        Q(1, 0)
-        MM(3, 3, [1])
-        M(2, 2)
-        MM(1, 3, [0])
-        MM(3, 2, [2])
-        MM(1, 3, [1])
-        MM(3, 2, [3])
-        M(2, 4)
-        MM(1, 3, [2])
-        MM(3, 2, [1])
-        MM(1, 2, [3])
-        BI(1, 3, "S")
-        MM(3, 3, [0])
-        Q(2, 1)
-        BI(1, 2, "V")
-        T(0, 4)
-        T(0, 0)
-        BQ(0, 3)
-        MM(2, 3, [3])
-        Q(2, 2)
-        BI(0, 2, "S")
-        MM(1, 3, [4])
-        BQ(1, 2)
-        MM(2, 2, [2])
-        MM(3, 3, [4])
-        BQ(1, 3)
-        MM(1, 2, [0])
-        MM(2, 3, [2])
-        BI(0, 1, "V")
-        MM(3, 2, [5])
-        MM(3, 3, [5])
-        MM(1, 2, [1])
-        MM(2, 2, [1])
-        L(0, 0)
-        MM(1, 3, [5])
-        BQ(0, 2)
-        MM(2, 2, [3])
-        MM(2, 3, [5])
-        ADD(3, 3)
-        MM(2, 3, [1])
-        BI(1, 1, "S")
-        MM(2, 3, [4])
-        BQ(0, 1)
-        MM(2, 2, [5])
-        MM(3, 2, [4])
-        ADD(2, 3)
-        MM(2, 2, [4])
-        MM(2, 1, [4])
-        ADD(3, 2)
-        MM(1, 2, [4, 5])
-        ADD(2, 2)
-        MM(1, 1, [4])
-        MM(3, 1, [4])
-        L(0, 4)
-        ADD(1, 2)
-        MM(1, 1, [0])
-        MM(2, 1, [1])
-        BQ(1, 1)
-        MM(2, 1, [3, 2])
-        ADD(1, 3)
-        MM(2, 1, [0, 5])
+        T(3, 4)
+        L(3, 2)
+        Q(3, 0)
         Q(0, 1)
-        MM(1, 1, [2])
-        ADD(2, 1)
-        MM(3, 1, [0])
-        MM(1, 1, [5])
-        M(0, 4)
-        MM(3, 1, [2])
-        SIG(1, 2)
-        MM(1, 0, [0])
-        MM(0, 3, [2])
-        SIG(1, 3)
-        MM(0, 2, [2])
+        L(3, 4)
+        T(0, 0)
+        M(3, 2)
+        L(0, 0)
+        T(2, 2)
+        M(3, 4)
+        L(2, 2)
+        T(2, 0)
+        Q(3, 1)
         M(0, 0)
-        MM(3, 1, [3])
-        SIG(3, 3)
-        MM(1, 1, [1, 3])
-        SIG(3, 2)
-        MM(3, 1, [1])
-        Q(0, 2)
-        MM(0, 3, [3])
-        SIG(2, 1)
+        L(2, 0)
+        T(2, 4)
+        M(2, 2)
+        L(2, 4)
+        T(0, 4)
         Q(0, 0)
-        MM(3, 1, [5])
-        MM(0, 1, [5])
-        SIG(2, 2)
-        ADD(3, 1)
-        MM(0, 2, [5])
-        MM(0, 1, [4])
-        SIG(2, 3)
-        ADD(1, 1)
-        MM(0, 2, [4])
-        MM(0, 1, [3])
-        SIG(3, 1)
-        BI(0, 0, "V")
-        MM(0, 1, [1])
+        Q(2, 1)
+        MM(0, 3, [2])
         MM(0, 2, [0])
-        BI(1, 0, "S")
-        MM(0, 1, [0, 2])
+        L(0, 4)
+        Q(3, 2)
+        MM(3, 3, [2])
+        M(2, 0)
+        MM(2, 2, [2])
+        MM(2, 3, [2])
+        MM(3, 3, [3])
+        BI(1, 3, "S")
         MM(0, 2, [3])
-        ADD(0, 1)
-        MM(0, 2, [1])
+        M(2, 4)
         MM(0, 3, [1])
-        BQ(0, 0)
-        MM(0, 3, [0, 5])
-        ADD(0, 2)
+        MM(3, 3, [1])
+        T(1, 2)
+        M(0, 4)
+        T(1, 0)
+        MM(0, 3, [0])
+        L(1, 2)
+        Q(2, 0)
+        MM(0, 2, [1])
+        MM(3, 2, [3])
+        Q(2, 2)
+        MM(3, 2, [1])
+        BQ(3)
+        MM(2, 2, [3])
+        L(1, 0)
+        MM(3, 2, [0])
+        MM(0, 2, [2])
+        MM(2, 3, [1])
+        Q(0, 2)
+        BI(0, 2, "S")
+        MM(3, 3, [4])
+        M(1, 0)
+        MM(2, 3, [3, 5])
+        MM(2, 2, [1])
+        MM(3, 3, [0])
+        BI(1, 2, "V")
+        MM(0, 3, [3])
+        T(1, 4)
+        BI(0, 1, "S")
+        MM(3, 3, [5])
+        Q(1, 0)
+        MM(2, 3, [0, 4])
+        BQ(2)
+        MM(0, 3, [5])
+        MM(3, 2, [2])
         MM(0, 3, [4])
-        MM(1, 0, [2])
-        SIG(0, 1)
+        ADD(2, 3)
+        MM(0, 2, [5])
+        MM(3, 2, [4])
+        L(1, 4)
         ADD(0, 3)
-        MM(1, 0, [4])
-        MM(0, 0, [1])
-        SIG(0, 2)
-        BQ(1, 0)
-        MM(2, 0, [0])
-        MM(1, 0, [3])
-        SIG(0, 3)
-        MM(1, 0, [1])
-        MM(0, 0, [4])
-        SIG(1, 1)
-        MM(2, 0, [3])
-        MM(1, 0, [5])
-        MM(2, 0, [1])
-        ADD(1, 0)
-        MM(0, 0, [3])
-        MM(2, 0, [5])
-        MM(0, 0, [5])
-        SIG(1, 0)
-        MM(2, 0, [2, 4])
-        MM(0, 0, [2])
-        ADD(2, 0)
+        MM(3, 2, [5])
+        MM(2, 2, [5])
+        ADD(3, 3)
+        MM(0, 2, [4])
+        MM(2, 2, [4])
+        BI(1, 1, "S")
+        ADD(3, 2)
+        MM(1, 3, [0])
+        MM(1, 2, [0])
+        MM(2, 2, [0])
+        ADD(0, 2)
+        MM(1, 1, [1, 0])
+        M(1, 2)
+        MM(1, 3, [1])
+        MM(3, 1, [3, 1, 0])
+        ADD(2, 2)
+        MM(0, 0, [2, 3])
+        Q(1, 1)
         MM(0, 0, [0])
-        MM(3, 0, [5])
+        BQ(1)
+        MM(2, 1, [1])
+        MM(1, 1, [3])
+        MM(3, 1, [2])
+        SIG(2, 3)
+        MM(1, 1, [2])
+        MM(0, 0, [1])
+        M(1, 4)
+        SIG(2, 2)
+        MM(3, 1, [4, 5])
+        SIG(3, 3)
+        MM(1, 3, [2])
+        MM(1, 2, [2])
+        ADD(3, 1)
+        SIG(3, 2)
+        MM(1, 3, [3])
+        MM(1, 2, [3])
+        Q(1, 2)
+        SIG(0, 2)
+        MM(1, 2, [1])
+        BI(1, 0, "V")
+        MM(0, 1, [4])
+        SIG(0, 3)
+        MM(1, 2, [4, 5])
+        MM(1, 1, [5])
+        SIG(3, 1)
+        MM(0, 1, [1])
+        ADD(1, 2)
+        MM(1, 1, [4])
+        BI(0, 0, "S")
+        MM(1, 3, [4, 5])
+        ADD(1, 1)
+        MM(2, 0, [0])
+        MM(2, 1, [0])
+        ADD(1, 3)
+        MM(0, 1, [3, 5])
+        MM(2, 1, [3])
+        MM(0, 1, [0])
+        MM(2, 0, [3])
+        SIG(1, 2)
+        BQ(0)
+        MM(0, 1, [2])
+        MM(2, 1, [2])
+        SIG(1, 1)
+        MM(2, 0, [1])
+        SIG(1, 3)
+        ADD(0, 1)
+        MM(0, 0, [4, 5])
+        MM(2, 1, [4])
+        SIG(0, 1)
         ADD(0, 0)
-        MM(3, 0, [2])
-        SIG(2, 0)
-        MM(3, 0, [1, 0])
+        MM(2, 1, [5])
+        MM(2, 0, [2, 4])
+        ADD(2, 1)
         SIG(0, 0)
-        MM(3, 0, [4, 3])
+        MM(2, 0, [5])
+        MM(3, 0, [1])
+        ADD(2, 0)
+        SIG(2, 1)
+        MM(3, 0, [2])
+        MM(1, 0, [4])
+        MM(3, 0, [3])
+        SIG(2, 0)
+        MM(1, 0, [0])
+        MM(3, 0, [0])
+        MM(1, 0, [3])
+        MM(3, 0, [5, 4])
+        MM(1, 0, [5])
         ADD(3, 0)
+        MM(1, 0, [2, 1])
         SIG(3, 0)
+        ADD(1, 0)
+        SIG(1, 0)

@@ -21,8 +21,6 @@ NN = 4
 NG = 6
 W = 512
 
-Z_BANKS = 6
-
 
 def tile_probabilistic_visual_hull_s1_kernel(
     tc, ratio, conf, rig_words, rig_scales, roam, prior, out_0, out_1
@@ -38,15 +36,11 @@ def tile_probabilistic_visual_hull_s1_kernel(
         rows = keep.tile([P, 512], BF16, name="rows")
         nc.gpsimd.memset(rows[:].bitcast(F32), 0.0)
         make_identity(nc, ident[:])
-        nc.scalar.dma_start(out=rows[0:4, :], in_=conf[0:2048].rearrange("(g c) -> g c", g=4))
-        nc.scalar.dma_start(out=rows[4:6, :], in_=conf[2048:3072].rearrange("(g c) -> g c", g=2))
-        nc.scalar.dma_start(out=rows[8:12, :], in_=prior.rearrange("(r c) -> r c", r=4))
         warm = keep.tile([P, 2], F32, name="warm")
         nc.vector.memset(warm[:, 0:1], 1.0)
         nc.scalar.activation(out=warm[:, 1:2], in_=warm[:, 0:1], func=ACT.Ln)
-        planes = [keep.tile([P, 4, 1024], U8, name="planes%d" % h, align_bytes=64) for h in range(2)]
-        for h in range(2):
-            nc.vector.memset(planes[h][:].rearrange("p g n -> p (g n)").bitcast(I32), 0)
+        planes = keep.tile([P, 4, VOX], U8, name="planes", align_bytes=64)
+        nc.vector.memset(planes[:].rearrange("p g n -> p (g n)").bitcast(I32), 0)
 
         ratio_sb = [keep.tile([P, RIG + ROAM], BF16, name="ratio%d" % f, align_bytes=64) for f in range(NF)]
         words = {}
@@ -55,6 +49,11 @@ def tile_probabilistic_visual_hull_s1_kernel(
         def load_ratio(f, g0, g1):
             c = slice(512 * g0, 512 * g1)
             nc.sync.dma_start(out=ratio_sb[f][:, c], in_=ratio[P * f : P * (f + 1), c])
+
+        def load_consts():
+            nc.sync.dma_start(out=rows[0:4, :], in_=conf[0:2048].rearrange("(g c) -> g c", g=4))
+            nc.sync.dma_start(out=rows[4:6, :], in_=conf[2048:3072].rearrange("(g c) -> g c", g=2))
+            nc.sync.dma_start(out=rows[8:12, :], in_=prior.rearrange("(r c) -> r c", r=4))
 
         def load_raw(g, n0, n1):
             t = keep.tile([P, 4, W * (n1 - n0)], BF16, name="raw%d_%d" % (g, n0), align_bytes=64)
@@ -65,20 +64,16 @@ def tile_probabilistic_visual_hull_s1_kernel(
             for n in range(n0, n1):
                 raw[g, n] = t[:, :, W * (n - n0) : W * (n - n0 + 1)]
 
-        def load_words(n0, n1):
-            t = keep.tile([P, 4, 2 * W * (n1 - n0)], U8, name="words%d" % n0, align_bytes=64)
-            nc.sync.dma_start(
-                out=t[:].bitcast(I32),
-                in_=rig_words[:, :, 2 * W * n0 : 2 * W * n1].rearrange("g p b -> p g b").bitcast(I32),
-            )
-            for n in range(n0, n1):
-                words[n] = t[:, :, 2 * W * (n - n0) : 2 * W * (n - n0 + 1)]
+        def load_words(g):
+            t = keep.tile([P, 2 * VOX], U8, name="words%d" % g, align_bytes=64)
+            nc.sync.dma_start(out=t[:].bitcast(I32), in_=rig_words[g].bitcast(I32))
+            words[g] = t
 
-        def load_scales(h):
+        def load_scales():
             for r in range(4):
                 nc.sync.dma_start(
-                    out=planes[h][r:P:32, :, :].bitcast(I32),
-                    in_=rig_scales[:, r:16:4, 1024 * h : 1024 * (h + 1)].rearrange("g q n -> q g n").bitcast(I32),
+                    out=planes[r:P:32, :, :].bitcast(I32),
+                    in_=rig_scales[:, r:16:4, :].rearrange("g q n -> q g n").bitcast(I32),
                 )
 
         e_codes = [keep.tile([P, NG, P], U32, name="ec%d" % f, align_bytes=64) for f in range(NF)]
@@ -89,15 +84,13 @@ def tile_probabilistic_visual_hull_s1_kernel(
         prior_w = keep.tile([P, 4, 2], F32, name="prior_w")
         prior_sb = keep.tile([P, VOX], BF16, name="prior_sb")
 
-        tfree = [0, 1]
+        free = ["b%d" % k for k in range(8)]
         tname = {}
-
-        def tbank():
-            return tfree.pop(0)
 
         def consts_a():
             cw = rows[:].bitcast(F32)
-            ct = psum.tile([P, 2, P], F32, name="ct", tag="z3")
+            k = free.pop(0)
+            ct = psum.tile([P, 2, P], F32, name="ct", tag=k)
             for u in range(2):
                 nc.tensor.transpose(ct[:, u, :], cw[:, u:256:2], ident[:])
             nc.vector.tensor_copy(
@@ -105,40 +98,42 @@ def tile_probabilistic_visual_hull_s1_kernel(
                 in_=ct[:, :, 0:6].rearrange("p u g -> p g u"),
             )
             nc.vector.tensor_copy(out=prior_w[:], in_=ct[:, :, 8:12].rearrange("p u r -> p r u"))
+            free.append(k)
 
         pts = []
 
         def consts_b(h):
-            pt = psum.tile([P, 2, 2, P], F32, name="pt", tag="z%d" % (5 - h))
+            k = free.pop(0)
+            pt = psum.tile([P, 2, 2, P], F32, name="pt", tag=k)
             for r in range(2):
                 for u in range(2):
                     nc.tensor.transpose(
                         pt[:, r, u, :], prior_w[:, 2 * h + r, u : u + 1].to_broadcast([P, P]), ident[:]
                     )
-            pts.append(pt)
+            pts.append((pt, k))
 
         def XC(eng):
             for h in range(2):
                 dst = prior_sb[:, 1024 * h : 1024 * (h + 1)].bitcast(F32).rearrange("p (r q u) -> p r q u", r=2, u=2)
-                src = pts[h][:].rearrange("p r u q -> p r q u")
+                src = pts[h][0][:].rearrange("p r u q -> p r q u")
                 if eng == "V":
                     nc.vector.tensor_copy(out=dst, in_=src)
                 else:
                     nc.scalar.copy(out=dst, in_=src)
+                free.append(pts[h][1])
 
         tb = {}
         lnt = {}
         eg = {}
         bg = {}
         zb = {}
-        free = list(range(Z_BANKS))
         zbank = {}
         done = {}
 
         def T(f, g0, ng=2):
-            k = tbank()
+            k = free.pop(0)
             tname[f, g0] = k
-            xt = psum.tile([P, 2, ng, P], F32, name="xt", tag="t%d" % k)
+            xt = psum.tile([P, 2, ng, P], F32, name="xt", tag=k)
             w = ratio_sb[f][:].bitcast(F32)
             for g in range(ng):
                 for u in range(2):
@@ -154,12 +149,12 @@ def tile_probabilistic_visual_hull_s1_kernel(
                 func=ACT.Ln,
             )
             lnt[f, g0] = ln
-            tfree.append(tname[f, g0])
+            free.append(tname[f, g0])
 
         def M(f, g0, ng=2):
             gp = g0 // 2
             if (f, gp) not in eg:
-                eg[f, gp] = work.tile([P, 2, P, 4], BF16, name="eg", bufs=6, align_bytes=64)
+                eg[f, gp] = work.tile([P, 2, P, 4], BF16, name="eg", bufs=5, align_bytes=64)
             nc.vector.tensor_tensor(
                 out=eg[f, gp][:, g0 % 2 : g0 % 2 + ng],
                 in0=lnt[f, g0][:],
@@ -196,15 +191,15 @@ def tile_probabilistic_visual_hull_s1_kernel(
                 if (f, n) not in zb:
                     k = free.pop(0)
                     zbank[f, n] = k
-                    zb[f, n] = psum.tile([P, W], F32, name="acc", tag="z%d" % k)
+                    zb[f, n] = psum.tile([P, W], F32, name="acc", tag=k)
                     done[f, n] = 0
                 first = done[f, n] == 0
                 done[f, n] += 1
                 last = done[f, n] == NG
                 cols = slice(W * n, W * (n + 1))
                 if g < 4:
-                    rhs = words[n][:, g, :].bitcast(E2M1X4)
-                    rsc = planes[n // 2][:, g, W * (n % 2) : W * (n % 2 + 1)]
+                    rhs = words[g][:, 2 * W * n : 2 * W * (n + 1)].bitcast(E2M1X4)
+                    rsc = planes[:, g, cols]
                 else:
                     rhs = b_codes[n][:, g - 4, :].bitcast(E4M3X4)
                     rsc = b_scales[n][:, g - 4, :]
@@ -225,7 +220,7 @@ def tile_probabilistic_visual_hull_s1_kernel(
         def out_tile(tiles, f, n, kind):
             h = n // 2
             if (f, h) not in tiles:
-                tiles[f, h] = work.tile([P, 2 * W], F32, name=kind, bufs=6)
+                tiles[f, h] = work.tile([P, 2 * W], F32, name=kind, bufs=7)
             return tiles[f, h]
 
         def store(tiles, dst, f, n, kind):
@@ -263,206 +258,202 @@ def tile_probabilistic_visual_hull_s1_kernel(
             )
             store(ot, out_1, f, n, "o")
 
-        SINGLE = {(1, 0), (3, 0)}
-        load_ratio(3, 0, 1)
-        load_ratio(3, 1, 2)
-        load_ratio(0, 2, 4)
-        load_raw(0, 3, 4)
-        load_ratio(3, 2, 4)
-        load_ratio(0, 0, 2)
-        load_ratio(3, 4, 6)
-        load_ratio(0, 4, 6)
-        load_ratio(2, 0, 6)
-        load_scales(1)
-        load_words(2, 4)
-        load_raw(1, 3, 4)
-        load_ratio(1, 0, 4)
-        load_raw(0, 1, 3)
-        load_raw(1, 2, 3)
-        load_ratio(1, 4, 6)
-        load_raw(1, 1, 2)
-        load_scales(0)
-        load_words(0, 2)
-        load_raw(0, 0, 1)
-        load_raw(1, 0, 1)
+        SINGLE = {(1, 0), (1, 1)}
+        load_ratio(3, 0, 2)
+        load_consts()
+        load_ratio(2, 0, 2)
+        load_ratio(0, 0, 6)
+        load_ratio(3, 2, 6)
+        load_ratio(2, 2, 6)
+        load_raw(0, 0, 2)
+        load_raw(1, 0, 2)
+        load_ratio(1, 0, 6)
+        load_scales()
+        load_words(1)
+        load_words(0)
+        load_words(2)
+        load_words(3)
+        load_raw(0, 2, 4)
+        load_raw(1, 2, 4)
         T(3, 0, 1)
         consts_a()
         T(3, 1, 1)
         L(3, 0, 1)
         L(3, 1, 1)
-        T(0, 2)
+        T(2, 0)
         M(3, 0, 1)
         M(3, 1, 1)
-        L(0, 2)
-        BI(0, 3, "V")
+        L(2, 0)
+        T(0, 4)
+        M(2, 0)
         consts_b(0)
+        T(0, 2)
+        L(0, 4)
         consts_b(1)
-        T(3, 2)
-        XC("S")
-        M(0, 2)
-        T(3, 4)
-        L(3, 2)
-        Q(3, 0)
-        Q(0, 1)
-        L(3, 4)
         T(0, 0)
-        M(3, 2)
-        L(0, 0)
+        Q(3, 0)
+        Q(2, 0)
+        L(0, 2)
+        T(3, 4)
+        M(0, 4)
+        T(2, 4)
+        L(3, 4)
+        M(0, 2)
         T(2, 2)
+        L(2, 4)
         M(3, 4)
         L(2, 2)
-        T(2, 0)
-        Q(3, 1)
-        M(0, 0)
-        L(2, 0)
-        T(2, 4)
-        M(2, 2)
-        L(2, 4)
-        T(0, 4)
-        Q(0, 0)
-        Q(2, 1)
-        MM(0, 3, [2])
-        MM(0, 2, [0])
-        L(0, 4)
-        Q(3, 2)
-        MM(3, 3, [2])
-        M(2, 0)
-        MM(2, 2, [2])
-        MM(2, 3, [2])
-        MM(3, 3, [3])
-        BI(1, 3, "S")
-        MM(0, 2, [3])
+        T(3, 2)
         M(2, 4)
-        MM(0, 3, [1])
-        MM(3, 3, [1])
-        T(1, 2)
-        M(0, 4)
-        T(1, 0)
-        MM(0, 3, [0])
-        L(1, 2)
-        Q(2, 0)
-        MM(0, 2, [1])
-        MM(3, 2, [3])
-        Q(2, 2)
-        MM(3, 2, [1])
-        BQ(3)
-        MM(2, 2, [3])
-        L(1, 0)
-        MM(3, 2, [0])
-        MM(0, 2, [2])
-        MM(2, 3, [1])
-        Q(0, 2)
-        BI(0, 2, "S")
-        MM(3, 3, [4])
-        M(1, 0)
-        MM(2, 3, [3, 5])
-        MM(2, 2, [1])
-        MM(3, 3, [0])
-        BI(1, 2, "V")
-        MM(0, 3, [3])
-        T(1, 4)
         BI(0, 1, "S")
-        MM(3, 3, [5])
-        Q(1, 0)
-        MM(2, 3, [0, 4])
-        BQ(2)
-        MM(0, 3, [5])
-        MM(3, 2, [2])
-        MM(0, 3, [4])
-        ADD(2, 3)
-        MM(0, 2, [5])
-        MM(3, 2, [4])
+        Q(3, 2)
+        M(2, 2)
+        BI(1, 1, "V")
+        L(3, 2)
+        Q(0, 2)
+        T(1, 2)
+        BQ(1)
+        L(0, 0)
+        T(1, 0)
+        Q(2, 2)
+        L(1, 2)
+        M(0, 0)
+        MM(3, 1, [5])
+        MM(2, 1, [5, 4])
+        MM(3, 1, [4])
+        XC("S")
+        MM(0, 1, [5])
+        M(3, 2)
+        T(1, 4)
+        BI(0, 0, "S")
+        Q(2, 1)
+        MM(0, 1, [4])
+        Q(3, 1)
+        MM(2, 0, [1])
+        MM(2, 1, [1])
+        Q(0, 0)
+        MM(3, 1, [1])
+        BI(1, 0, "V")
+        MM(3, 0, [1, 0])
+        MM(0, 0, [0])
+        MM(0, 1, [0])
+        L(1, 0)
+        MM(3, 1, [0])
+        Q(0, 1)
+        MM(2, 1, [0])
+        BQ(0)
+        MM(3, 1, [2])
+        MM(0, 0, [1])
         L(1, 4)
+        MM(0, 1, [2, 1])
+        MM(2, 1, [2])
+        M(1, 2)
+        MM(3, 1, [3])
+        MM(2, 1, [3])
+        MM(0, 0, [3])
+        MM(3, 0, [3])
+        ADD(3, 1)
+        MM(0, 1, [3])
+        MM(3, 0, [4])
+        ADD(2, 1)
+        MM(3, 0, [5, 2])
+        SIG(3, 1)
+        MM(0, 2, [0])
+        ADD(0, 1)
+        MM(0, 0, [4])
+        BI(0, 3, "S")
+        MM(2, 0, [2])
+        ADD(3, 0)
+        MM(0, 3, [3, 2])
+        BI(0, 2, "V")
+        MM(0, 0, [5])
+        MM(2, 0, [0])
+        MM(0, 0, [2])
+        MM(0, 3, [1])
+        MM(2, 3, [3])
+        ADD(0, 0)
+        MM(2, 0, [5])
+        SIG(3, 0)
+        MM(2, 3, [1])
+        BI(1, 3, "V")
+        MM(3, 3, [0])
+        BI(1, 2, "S")
+        MM(2, 0, [4, 3])
+        MM(0, 3, [0])
+        MM(0, 2, [2])
+        ADD(2, 0)
+        MM(3, 2, [3])
+        MM(3, 3, [1])
+        MM(3, 2, [2])
+        BQ(3)
+        MM(3, 2, [1])
+        MM(0, 2, [3])
+        SIG(2, 1)
+        MM(3, 3, [2])
+        MM(2, 3, [0])
+        SIG(2, 0)
+        BQ(2)
+        MM(0, 2, [1])
+        MM(2, 2, [2])
+        SIG(0, 1)
+        MM(2, 3, [2])
+        MM(2, 2, [3])
+        SIG(0, 0)
+        M(1, 0)
+        MM(0, 3, [5, 4])
+        MM(3, 3, [5])
+        MM(0, 2, [5, 4])
         ADD(0, 3)
-        MM(3, 2, [5])
-        MM(2, 2, [5])
-        ADD(3, 3)
-        MM(0, 2, [4])
-        MM(2, 2, [4])
-        BI(1, 1, "S")
-        ADD(3, 2)
-        MM(1, 3, [0])
-        MM(1, 2, [0])
+        MM(3, 2, [4])
         MM(2, 2, [0])
         ADD(0, 2)
-        MM(1, 1, [1, 0])
-        M(1, 2)
-        MM(1, 3, [1])
-        MM(3, 1, [3, 1, 0])
-        ADD(2, 2)
-        MM(0, 0, [2, 3])
-        Q(1, 1)
-        MM(0, 0, [0])
-        BQ(1)
-        MM(2, 1, [1])
-        MM(1, 1, [3])
-        MM(3, 1, [2])
-        SIG(2, 3)
-        MM(1, 1, [2])
-        MM(0, 0, [1])
-        M(1, 4)
-        SIG(2, 2)
-        MM(3, 1, [4, 5])
-        SIG(3, 3)
-        MM(1, 3, [2])
-        MM(1, 2, [2])
-        ADD(3, 1)
-        SIG(3, 2)
-        MM(1, 3, [3])
-        MM(1, 2, [3])
-        Q(1, 2)
-        SIG(0, 2)
-        MM(1, 2, [1])
-        BI(1, 0, "V")
-        MM(0, 1, [4])
+        MM(3, 3, [3])
         SIG(0, 3)
+        MM(3, 3, [4])
+        Q(1, 0)
+        MM(2, 3, [5])
+        SIG(0, 2)
+        ADD(3, 3)
+        MM(3, 2, [5, 0])
+        MM(1, 2, [0])
+        Q(1, 1)
+        MM(2, 3, [4])
+        SIG(3, 3)
+        ADD(3, 2)
+        MM(2, 2, [1])
+        MM(1, 1, [0])
+        ADD(2, 3)
+        MM(2, 2, [4])
+        SIG(3, 2)
+        MM(1, 0, [1])
+        MM(1, 3, [3])
+        M(1, 4)
+        SIG(2, 3)
+        MM(2, 2, [5])
+        MM(1, 3, [2])
+        MM(1, 0, [0])
+        MM(1, 2, [1])
+        ADD(2, 2)
+        MM(1, 0, [3])
+        MM(1, 2, [2])
+        Q(1, 2)
+        MM(1, 3, [0])
+        SIG(2, 2)
+        MM(1, 3, [1])
+        MM(1, 0, [2])
+        MM(1, 3, [5, 4])
+        MM(1, 0, [4])
+        ADD(1, 3)
+        MM(1, 0, [5])
         MM(1, 2, [4, 5])
+        ADD(1, 0)
+        MM(1, 2, [3])
+        SIG(1, 3)
         MM(1, 1, [5])
-        SIG(3, 1)
-        MM(0, 1, [1])
         ADD(1, 2)
         MM(1, 1, [4])
-        BI(0, 0, "S")
-        MM(1, 3, [4, 5])
-        ADD(1, 1)
-        MM(2, 0, [0])
-        MM(2, 1, [0])
-        ADD(1, 3)
-        MM(0, 1, [3, 5])
-        MM(2, 1, [3])
-        MM(0, 1, [0])
-        MM(2, 0, [3])
-        SIG(1, 2)
-        BQ(0)
-        MM(0, 1, [2])
-        MM(2, 1, [2])
-        SIG(1, 1)
-        MM(2, 0, [1])
-        SIG(1, 3)
-        ADD(0, 1)
-        MM(0, 0, [4, 5])
-        MM(2, 1, [4])
-        SIG(0, 1)
-        ADD(0, 0)
-        MM(2, 1, [5])
-        MM(2, 0, [2, 4])
-        ADD(2, 1)
-        SIG(0, 0)
-        MM(2, 0, [5])
-        MM(3, 0, [1])
-        ADD(2, 0)
-        SIG(2, 1)
-        MM(3, 0, [2])
-        MM(1, 0, [4])
-        MM(3, 0, [3])
-        SIG(2, 0)
-        MM(1, 0, [0])
-        MM(3, 0, [0])
-        MM(1, 0, [3])
-        MM(3, 0, [5, 4])
-        MM(1, 0, [5])
-        ADD(3, 0)
-        MM(1, 0, [2, 1])
-        SIG(3, 0)
-        ADD(1, 0)
         SIG(1, 0)
+        MM(1, 1, [2, 3, 1])
+        SIG(1, 2)
+        ADD(1, 1)
+        SIG(1, 1)

from contextlib import ExitStack

import concourse.mybir as mybir
from concourse.masks import make_identity

F32 = mybir.dt.float32
BF16 = mybir.dt.bfloat16
I32 = mybir.dt.int32
U32 = mybir.dt.uint32
U8 = mybir.dt.uint8
E4M3X4 = mybir.dt.float8_e4m3fn_x4
E2M1X4 = mybir.dt.float4_e2m1fn_x4
ACT = mybir.ActivationFunctionType
ALU = mybir.AluOpType

FRAMES, RIG, ROAM, VOX = 512, 2048, 1024, 2048
FLOPS = 2 * FRAMES * (RIG + ROAM) * VOX
P = 128
NF = 4
NN = 4
NG = 6
W = 512


def tile_probabilistic_visual_hull_s1_kernel(
    tc, ratio, conf, rig_words, rig_scales, roam, prior, out_0, out_1
):
    nc = tc.nc
    with ExitStack() as ctx:
        keep = ctx.enter_context(tc.tile_pool(name="keep", bufs=1))
        work = ctx.enter_context(tc.tile_pool(name="work", bufs=3))
        psum = ctx.enter_context(tc.psum_pool(name="psum", bufs=1))
        ctx.enter_context(tc.manual_schedule())

        ident = keep.tile([P, P], F32, name="ident")
        rows = keep.tile([P, 512], BF16, name="rows")
        nc.gpsimd.memset(rows[:].bitcast(F32), 0.0)
        make_identity(nc, ident[:])
        warm = keep.tile([P, 2], F32, name="warm")
        nc.vector.memset(warm[:, 0:1], 1.0)
        nc.scalar.activation(out=warm[:, 1:2], in_=warm[:, 0:1], func=ACT.Ln)
        planes = keep.tile([P, 4, VOX], U8, name="planes", align_bytes=64)
        nc.vector.memset(planes[:].rearrange("p g n -> p (g n)").bitcast(I32), 0)

        ratio_sb = [keep.tile([P, RIG + ROAM], BF16, name="ratio%d" % f, align_bytes=64) for f in range(NF)]
        words = {}
        raw = {}

        def load_ratio(f, g0, g1):
            c = slice(512 * g0, 512 * g1)
            nc.sync.dma_start(out=ratio_sb[f][:, c], in_=ratio[P * f : P * (f + 1), c])

        def load_consts():
            nc.sync.dma_start(out=rows[0:4, :], in_=conf[0:2048].rearrange("(g c) -> g c", g=4))
            nc.sync.dma_start(out=rows[4:6, :], in_=conf[2048:3072].rearrange("(g c) -> g c", g=2))
            nc.sync.dma_start(out=rows[8:12, :], in_=prior.rearrange("(r c) -> r c", r=4))

        def load_raw(g, n0, n1):
            t = keep.tile([P, 4, W * (n1 - n0)], BF16, name="raw%d_%d" % (g, n0), align_bytes=64)
            nc.sync.dma_start(
                out=t[:],
                in_=roam[512 * g : 512 * (g + 1), W * n0 : W * n1].rearrange("(p j) n -> p j n", j=4),
            )
            for n in range(n0, n1):
                raw[g, n] = t[:, :, W * (n - n0) : W * (n - n0 + 1)]

        def load_words(g):
            t = keep.tile([P, 2 * VOX], U8, name="words%d" % g, align_bytes=64)
            nc.sync.dma_start(out=t[:].bitcast(I32), in_=rig_words[g].bitcast(I32))
            words[g] = t

        def load_scales():
            for r in range(4):
                nc.sync.dma_start(
                    out=planes[r:P:32, :, :].bitcast(I32),
                    in_=rig_scales[:, r:16:4, :].rearrange("g q n -> q g n").bitcast(I32),
                )

        e_codes = [keep.tile([P, NG, P], U32, name="ec%d" % f, align_bytes=64) for f in range(NF)]
        e_scales = [keep.tile([P, NG, P], U8, name="es%d" % f, align_bytes=64) for f in range(NF)]
        b_codes = [keep.tile([P, 2, W], U32, name="bc%d" % n, align_bytes=64) for n in range(NN)]
        b_scales = [keep.tile([P, 2, W], U8, name="bs%d" % n, align_bytes=64) for n in range(NN)]
        conf_sb = keep.tile([P, NG, 4], BF16, name="conf_sb")
        prior_w = keep.tile([P, 4, 2], F32, name="prior_w")
        prior_sb = keep.tile([P, VOX], BF16, name="prior_sb")

        free = ["b%d" % k for k in range(8)]
        tname = {}

        def consts_a():
            cw = rows[:].bitcast(F32)
            k = free.pop(0)
            ct = psum.tile([P, 2, P], F32, name="ct", tag=k)
            for u in range(2):
                nc.tensor.transpose(ct[:, u, :], cw[:, u:256:2], ident[:])
            nc.vector.tensor_copy(
                out=conf_sb[:].rearrange("p g t -> p (g t)").bitcast(F32).rearrange("p (g u) -> p g u", u=2),
                in_=ct[:, :, 0:6].rearrange("p u g -> p g u"),
            )
            nc.vector.tensor_copy(out=prior_w[:], in_=ct[:, :, 8:12].rearrange("p u r -> p r u"))
            free.append(k)

        pts = []

        def consts_b(h):
            k = free.pop(0)
            pt = psum.tile([P, 2, 2, P], F32, name="pt", tag=k)
            for r in range(2):
                for u in range(2):
                    nc.tensor.transpose(
                        pt[:, r, u, :], prior_w[:, 2 * h + r, u : u + 1].to_broadcast([P, P]), ident[:]
                    )
            pts.append((pt, k))

        def XC(eng):
            for h in range(2):
                dst = prior_sb[:, 1024 * h : 1024 * (h + 1)].bitcast(F32).rearrange("p (r q u) -> p r q u", r=2, u=2)
                src = pts[h][0][:].rearrange("p r u q -> p r q u")
                if eng == "V":
                    nc.vector.tensor_copy(out=dst, in_=src)
                else:
                    nc.scalar.copy(out=dst, in_=src)
                free.append(pts[h][1])

        tb = {}
        lnt = {}
        eg = {}
        bg = {}
        zb = {}
        zbank = {}
        done = {}

        def T(f, g0, ng=2):
            k = free.pop(0)
            tname[f, g0] = k
            xt = psum.tile([P, 2, ng, P], F32, name="xt", tag=k)
            w = ratio_sb[f][:].bitcast(F32)
            for g in range(ng):
                for u in range(2):
                    base = 256 * (g0 + g)
                    nc.tensor.transpose(xt[:, u, g, :], w[:, base + u : base + 256 : 2], ident[:])
            tb[f, g0] = xt

        def L(f, g0, ng=2):
            ln = work.tile([P, ng, P, 4], F32, name="ln", bufs=6, align_bytes=64)
            nc.scalar.activation(
                out=ln[:].rearrange("p g r (u e) -> p (g r) u e", e=2),
                in_=tb[f, g0][:].rearrange("p u g r -> p (u g r)").bitcast(BF16).rearrange("p (u x e) -> p x u e", u=2, e=2),
                func=ACT.Ln,
            )
            lnt[f, g0] = ln
            free.append(tname[f, g0])

        def M(f, g0, ng=2):
            gp = g0 // 2
            if (f, gp) not in eg:
                eg[f, gp] = work.tile([P, 2, P, 4], BF16, name="eg", bufs=5, align_bytes=64)
            nc.vector.tensor_tensor(
                out=eg[f, gp][:, g0 % 2 : g0 % 2 + ng],
                in0=lnt[f, g0][:],
                in1=conf_sb[:, g0 : g0 + ng, :].unsqueeze(2).to_broadcast([P, ng, P, 4]),
                op=ALU.mult,
            )

        def Q(f, gp):
            nc.vector.quantize_mx(
                out=e_codes[f][:, 2 * gp : 2 * gp + 2, :].rearrange("p g r -> p (g r)").bitcast(E4M3X4),
                scales=e_scales[f][:, 2 * gp : 2 * gp + 2, :].rearrange("p g r -> p (g r)"),
                in_=eg[f, gp][:].rearrange("p g r t -> p (g r t)"),
            )

        def BI(g, n, eng):
            if n not in bg:
                bg[n] = work.tile([P, 2, W, 4], BF16, name="bg", bufs=3, align_bytes=64)
            dst = bg[n][:, g].rearrange("p (c i) t -> p c t i", i=4)
            src = raw[g, n].rearrange("p t (c i) -> p c t i", i=4)
            if eng == "V":
                nc.vector.tensor_copy(out=dst, in_=src)
            else:
                nc.scalar.copy(out=dst, in_=src)

        def BQ(n):
            nc.vector.quantize_mx(
                out=b_codes[n][:].rearrange("p g c -> p (g c)").bitcast(E4M3X4),
                scales=b_scales[n][:].rearrange("p g c -> p (g c)"),
                in_=bg[n][:].rearrange("p g c t -> p (g c t)"),
            )

        def MM(f, n, gs):
            for g in gs:
                if (f, n) not in zb:
                    k = free.pop(0)
                    zbank[f, n] = k
                    zb[f, n] = psum.tile([P, W], F32, name="acc", tag=k)
                    done[f, n] = 0
                first = done[f, n] == 0
                done[f, n] += 1
                last = done[f, n] == NG
                cols = slice(W * n, W * (n + 1))
                if g < 4:
                    rhs = words[g][:, 2 * W * n : 2 * W * (n + 1)].bitcast(E2M1X4)
                    rsc = planes[:, g, cols]
                else:
                    rhs = b_codes[n][:, g - 4, :].bitcast(E4M3X4)
                    rsc = b_scales[n][:, g - 4, :]
                nc.tensor.matmul_mx(
                    out=zb[f, n][:],
                    lhsT=e_codes[f][:, g, :].bitcast(E4M3X4),
                    lhsT_scale=e_scales[f][:, g, :],
                    rhs=rhs,
                    rhs_scale=rsc,
                    start=first,
                    stop=last,
                )

        zt = {}
        ot = {}
        half_done = {}

        def out_tile(tiles, f, n, kind):
            h = n // 2
            if (f, h) not in tiles:
                tiles[f, h] = work.tile([P, 2 * W], F32, name=kind, bufs=7)
            return tiles[f, h]

        def store(tiles, dst, f, n, kind):
            h = n // 2
            k = (kind, f, h)
            half_done[k] = half_done.get(k, 0) + 1
            if (f, h) in SINGLE:
                nc.sync.dma_start(
                    out=dst[P * f : P * (f + 1), W * n : W * (n + 1)],
                    in_=tiles[f, h][:, W * (n % 2) : W * (n % 2 + 1)],
                )
            elif half_done[k] == 2:
                nc.sync.dma_start(
                    out=dst[P * f : P * (f + 1), 2 * W * h : 2 * W * (h + 1)], in_=tiles[f, h][:]
                )

        def ADD(f, n):
            z = out_tile(zt, f, n, "z")
            nc.vector.tensor_tensor(
                out=z[:, W * (n % 2) : W * (n % 2 + 1)],
                in0=zb[f, n][:],
                in1=prior_sb[:, W * n : W * (n + 1)],
                op=ALU.add,
            )
            free.append(zbank[f, n])
            store(zt, out_0, f, n, "z")

        def SIG(f, n):
            o = out_tile(ot, f, n, "o")
            nc.scalar.activation(
                out=o[:, W * (n % 2) : W * (n % 2 + 1)],
                in_=zt[f, n // 2][:, W * (n % 2) : W * (n % 2 + 1)],
                func=ACT.Sigmoid,
                scale=-1.0,
            )
            store(ot, out_1, f, n, "o")

        SINGLE = {(1, 0), (1, 1)}
        load_ratio(3, 0, 2)
        load_consts()
        load_ratio(2, 0, 2)
        load_ratio(0, 0, 6)
        load_ratio(3, 2, 6)
        load_ratio(2, 2, 6)
        load_raw(0, 0, 2)
        load_raw(1, 0, 2)
        load_ratio(1, 0, 6)
        load_scales()
        load_words(1)
        load_words(0)
        load_words(2)
        load_words(3)
        load_raw(0, 2, 4)
        load_raw(1, 2, 4)
        T(3, 0, 1)
        consts_a()
        T(3, 1, 1)
        L(3, 0, 1)
        L(3, 1, 1)
        T(2, 0)
        M(3, 0, 1)
        M(3, 1, 1)
        L(2, 0)
        T(0, 4)
        M(2, 0)
        consts_b(0)
        T(0, 2)
        L(0, 4)
        consts_b(1)
        T(0, 0)
        Q(3, 0)
        Q(2, 0)
        L(0, 2)
        T(3, 4)
        M(0, 4)
        T(2, 4)
        L(3, 4)
        M(0, 2)
        T(2, 2)
        L(2, 4)
        M(3, 4)
        L(2, 2)
        T(3, 2)
        M(2, 4)
        BI(0, 1, "S")
        Q(3, 2)
        M(2, 2)
        BI(1, 1, "V")
        L(3, 2)
        Q(0, 2)
        T(1, 2)
        BQ(1)
        L(0, 0)
        T(1, 0)
        Q(2, 2)
        L(1, 2)
        M(0, 0)
        MM(3, 1, [5])
        MM(2, 1, [5, 4])
        MM(3, 1, [4])
        XC("S")
        MM(0, 1, [5])
        M(3, 2)
        T(1, 4)
        BI(0, 0, "S")
        Q(2, 1)
        MM(0, 1, [4])
        Q(3, 1)
        MM(2, 0, [1])
        MM(2, 1, [1])
        Q(0, 0)
        MM(3, 1, [1])
        BI(1, 0, "V")
        MM(3, 0, [1, 0])
        MM(0, 0, [0])
        MM(0, 1, [0])
        L(1, 0)
        MM(3, 1, [0])
        Q(0, 1)
        MM(2, 1, [0])
        BQ(0)
        MM(3, 1, [2])
        MM(0, 0, [1])
        L(1, 4)
        MM(0, 1, [2, 1])
        MM(2, 1, [2])
        M(1, 2)
        MM(3, 1, [3])
        MM(2, 1, [3])
        MM(0, 0, [3])
        MM(3, 0, [3])
        ADD(3, 1)
        MM(0, 1, [3])
        MM(3, 0, [4])
        ADD(2, 1)
        MM(3, 0, [5, 2])
        SIG(3, 1)
        MM(0, 2, [0])
        ADD(0, 1)
        MM(0, 0, [4])
        BI(0, 3, "S")
        MM(2, 0, [2])
        ADD(3, 0)
        MM(0, 3, [3, 2])
        BI(0, 2, "V")
        MM(0, 0, [5])
        MM(2, 0, [0])
        MM(0, 0, [2])
        MM(0, 3, [1])
        MM(2, 3, [3])
        ADD(0, 0)
        MM(2, 0, [5])
        SIG(3, 0)
        MM(2, 3, [1])
        BI(1, 3, "V")
        MM(3, 3, [0])
        BI(1, 2, "S")
        MM(2, 0, [4, 3])
        MM(0, 3, [0])
        MM(0, 2, [2])
        ADD(2, 0)
        MM(3, 2, [3])
        MM(3, 3, [1])
        MM(3, 2, [2])
        BQ(3)
        MM(3, 2, [1])
        MM(0, 2, [3])
        SIG(2, 1)
        MM(3, 3, [2])
        MM(2, 3, [0])
        SIG(2, 0)
        BQ(2)
        MM(0, 2, [1])
        MM(2, 2, [2])
        SIG(0, 1)
        MM(2, 3, [2])
        MM(2, 2, [3])
        SIG(0, 0)
        M(1, 0)
        MM(0, 3, [5, 4])
        MM(3, 3, [5])
        MM(0, 2, [5, 4])
        ADD(0, 3)
        MM(3, 2, [4])
        MM(2, 2, [0])
        ADD(0, 2)
        MM(3, 3, [3])
        SIG(0, 3)
        MM(3, 3, [4])
        Q(1, 0)
        MM(2, 3, [5])
        SIG(0, 2)
        ADD(3, 3)
        MM(3, 2, [5, 0])
        MM(1, 2, [0])
        Q(1, 1)
        MM(2, 3, [4])
        SIG(3, 3)
        ADD(3, 2)
        MM(2, 2, [1])
        MM(1, 1, [0])
        ADD(2, 3)
        MM(2, 2, [4])
        SIG(3, 2)
        MM(1, 0, [1])
        MM(1, 3, [3])
        M(1, 4)
        SIG(2, 3)
        MM(2, 2, [5])
        MM(1, 3, [2])
        MM(1, 0, [0])
        MM(1, 2, [1])
        ADD(2, 2)
        MM(1, 0, [3])
        MM(1, 2, [2])
        Q(1, 2)
        MM(1, 3, [0])
        SIG(2, 2)
        MM(1, 3, [1])
        MM(1, 0, [2])
        MM(1, 3, [5, 4])
        MM(1, 0, [4])
        ADD(1, 3)
        MM(1, 0, [5])
        MM(1, 2, [4, 5])
        ADD(1, 0)
        MM(1, 2, [3])
        SIG(1, 3)
        MM(1, 1, [5])
        ADD(1, 2)
        MM(1, 1, [4])
        SIG(1, 0)
        MM(1, 1, [2, 3, 1])
        SIG(1, 2)
        ADD(1, 1)
        SIG(1, 1)
